import numpy as np
import ml_dtypes


def mxq(x, axis, fmt="e4m3"):
    dtype, down = {"e4m3": (ml_dtypes.float8_e4m3fn, 7), "e5m2": (ml_dtypes.float8_e5m2, 14)}[fmt]
    v = np.moveaxis(np.asarray(x, np.float32).astype(ml_dtypes.bfloat16).astype(np.float64), axis, -1)
    blocks = v.reshape(v.shape[:-1] + (-1, 32))
    amax = np.abs(blocks).max(-1, keepdims=True)
    byte = np.maximum(np.where(amax > 0, np.frexp(amax)[1] - 1 + 127, 0) - down, 1)
    scale = np.exp2(byte - 127.0)
    codes = (blocks / scale).astype(np.float32).astype(dtype).astype(np.float64)
    return np.moveaxis((codes * scale).reshape(v.shape), -1, axis)


WIDE = False


def mx_kscale(k):
    if not WIDE:
        return np.ones(k)
    levels = np.array([10, -10, 5, -5, 0])
    if k % 512:
        return np.exp2(np.random.permutation(np.resize(levels, k // 32))).repeat(32)
    a = np.empty((k // 512, 16))
    for p in range(k // 512):
        a[p, :8] = np.random.permutation(np.resize(levels, 8))
        for g in range(8):
            far = levels[np.abs(levels - a[p, g]) >= 10]
            a[p, g + 8] = far[np.random.randint(len(far))]
    return np.exp2(a.ravel()).repeat(32)


def f64(x):
    return np.asarray(x).astype(np.float64)


def striped(idx):
    return np.tile(idx.reshape(-1, 16).T, (8, 1)).astype(np.uint16)


def unstriped(offs):
    return offs[:16].T.reshape(-1).astype(np.int64)


E2M1 = np.array([0.0, 0.5, 1.0, 1.5, 2.0, 3.0, 4.0, 6.0, -0.0, -0.5, -1.0, -1.5, -2.0, -3.0, -4.0, -6.0])


def pack_weight(w, fmt):
    k, n = w.shape
    w = f64(np.asarray(w, np.float32).astype(ml_dtypes.bfloat16)).reshape(k // 32, 32, n)
    amax = np.abs(w).max(1)
    if fmt == "e4m3":
        byte = np.frexp(amax)[1] - 1 + 127 - 7
    else:
        mant, ex = np.frexp(amax / 6.0)
        byte = np.where(mant > 0.5, ex, ex - 1) + 127
    byte = np.clip(np.where(amax > 0, byte, 1), 1, 254)
    scaled = (w * np.exp2(127.0 - byte)[:, None, :]).reshape(k, n).astype(np.float32)
    by_word = np.ascontiguousarray(scaled.reshape(k // 512, 128, 4, n).transpose(0, 1, 3, 2))
    if fmt == "e4m3":
        words = by_word.astype(ml_dtypes.float8_e4m3fn).view(np.uint8)
    else:
        c = by_word.astype(ml_dtypes.float4_e2m1fn).view(np.uint8) & 0xF
        words = (c[..., 0::2] | (c[..., 1::2] << 4)).reshape(k // 512, 128, 2 * n)
    return np.ascontiguousarray(words), np.ascontiguousarray(byte.astype(np.uint8).reshape(k // 512, 16, n))


def unpack_weight(words, scales, fmt):
    g, _, n = scales.shape
    words = np.ascontiguousarray(words).reshape(g, 128, n, -1)
    if fmt == "e4m3":
        vals = words.view(ml_dtypes.float8_e4m3fn).astype(np.float64)
    else:
        nib = np.empty((g, 128, n, 4), np.uint8)
        nib[..., 0::2] = words & 0xF
        nib[..., 1::2] = words >> 4
        vals = E2M1[nib]
    vals = vals * np.repeat(np.exp2(scales.astype(np.float64) - 127.0), 8, axis=1)[..., None]
    return vals.transpose(0, 1, 3, 2).reshape(g * 512, n)


def gelu(v):
    return 0.5 * v * (1.0 + np.tanh(np.sqrt(2.0 / np.pi) * (v + 0.044715 * v**3)))


def bf(x):
    return np.asarray(x, np.float32).astype(ml_dtypes.bfloat16)


def planes(Y):
    n, m = Y.shape
    b = f64(bf(Y)).reshape(n // 32, 32, m)
    amax = np.abs(b).max(1)
    byte = np.clip(np.where(amax > 0, np.frexp(amax)[1] - 1 + 127 - 7, 1), 1, 254)
    codes = (b * np.exp2(127.0 - byte)[:, None, :]).reshape(n, m).astype(np.float32).astype(ml_dtypes.float8_e4m3fn).view(np.uint8)
    words = codes.reshape(n // 512, 128, 4, m).transpose(0, 1, 3, 2)
    return np.ascontiguousarray(words), np.ascontiguousarray(byte.astype(np.uint8).reshape(n // 512, 16, m))


K, T, S, H, T2, N = 1536, 4096, 1024, 512, 2048, 512

def setup_inputs():
    n = np.random.standard_normal
    s = mx_kscale(K)[:, None]
    u = mx_kscale(H)[:, None]
    tab_words, tab_scales = pack_weight(n((K, T)) * s, "e4m3")
    wa_words, wa_scales = pack_weight(n((H, N)) / np.sqrt(H) / u, "e2m1")
    return {
        "tab_words": tab_words, "tab_scales": tab_scales,
        "offs": striped(np.random.permutation(T)[:S]),
        "offs2": striped(np.random.permutation(T2)[:S]),
        "w1": (n((K, H)) / np.sqrt(K) / s * u.T).astype(np.float32),
        "curve": (0.3 * n(H) / u[:, 0]).astype(np.float32),
        "wgs": np.exp(0.3 * n((128, S))).astype(np.float32),
        "page0": (n((H, T2)) * u).astype(np.float32),
        "wa_words": wa_words, "wa_scales": wa_scales,
        "wb": (n((H, N)) / np.sqrt(H) / u).astype(np.float32),
        "appeal": (0.5 * n(N)).astype(np.float32),
    }

def reference(tab_words, tab_scales, offs, offs2, w1, curve, wgs, page0, wa_words, wa_scales, wb, appeal):
    v = unpack_weight(tab_words, tab_scales, "e4m3")[:, unstriped(offs)]
    a = mxq(f64(w1), 0, "e4m3").T @ v
    h = a + f64(curve)[:, None] * (a * a)
    page = f64(page0).copy()
    page[:, unstriped(offs2)] = np.tile(f64(wgs), (H // 128, 1)) * h
    words, scales = planes(page)
    pq = mxq(page, 0, "e4m3")
    wa = unpack_weight(wa_words, wa_scales, "e2m1")
    fit = wa.T @ pq
    want = mxq(f64(wb), 0, "e4m3").T @ pq
    y = fit * want + f64(appeal)[:, None]
    return y, page, words, scales

@@ -1,0 +1,275 @@
+from contextlib import ExitStack
+
+import concourse.mybir as mybir
+
+K, T, S, H, T2, N = 1536, 4096, 1024, 512, 2048, 512
+FLOPS = 2 * K * H * S + 2 * 2 * H * N * T2
+
+F32 = mybir.dt.float32
+BF16 = mybir.dt.bfloat16
+I32 = mybir.dt.int32
+U32 = mybir.dt.uint32
+U16 = mybir.dt.uint16
+U8 = mybir.dt.uint8
+FP8X4 = mybir.dt.float8_e4m3fn_x4
+FP4X4 = mybir.dt.float4_e2m1fn_x4
+MULT = mybir.AluOpType.mult
+ADD = mybir.AluOpType.add
+IDENTITY = mybir.ActivationFunctionType.Identity
+
+P = 128
+PACK = 4
+K_PASS = P * PACK
+PASSES = K // K_PASS
+BANK = 512
+HALVES = S // BANK
+LIST_COLS = BANK // 16
+CHUNKS = [256, 256, 512, 512, 512]
+VECTOR_CHUNKS = 3
+SCALAR_ADD_EVERY = 4
+
+
+def tile_list_recipe_taste_store_kernel(
+    tc, tab_words, tab_scales, offs, offs2, w1, curve, wgs, page0, wa_words, wa_scales, wb, appeal,
+    out_0, out_1, out_2, out_3,
+):
+    nc = tc.nc
+    with ExitStack() as ctx:
+        keep = ctx.enter_context(tc.tile_pool(name="keep", bufs=1))
+        ring = ctx.enter_context(tc.tile_pool(name="ring", bufs=3))
+        psum = ctx.enter_context(tc.psum_pool(name="psum", bufs=8))
+
+        picks = keep.tile([P, S // 16], U16, name="picks")
+        places = keep.tile([P, S // 16], U16, name="places")
+        nc.sync.dma_start(picks[:], offs)
+
+        table_scales = keep.tile([P, T], U8, name="table_scales", align_bytes=64)
+        nc.vector.memset(table_scales[:].bitcast(I32), 0)
+        for q in range(4):
+            nc.gpsimd.dma_start(
+                out=table_scales[32 * q : 32 * q + 4 * PASSES, :].bitcast(I32),
+                in_=tab_scales[:, 4 * q : 4 * q + 4, :].bitcast(I32),
+            )
+        curve_cols = keep.tile([P, PACK], F32, name="curve_cols")
+        nc.gpsimd.dma_start(out=curve_cols[:], in_=curve.rearrange("(p t) -> p t", t=PACK))
+        wa_plane = keep.tile([P, N], U8, name="wa_plane", align_bytes=64)
+        nc.vector.memset(wa_plane[:].bitcast(I32), 0)
+        for q in range(4):
+            nc.gpsimd.dma_start(
+                out=wa_plane[32 * q : 32 * q + 4, :].bitcast(I32),
+                in_=wa_scales[0, 4 * q : 4 * q + 4, :].bitcast(I32),
+            )
+
+        table, w1_raw = [], []
+        for a in range(PASSES):
+            words = keep.tile([P, T], U32, name=f"table{a}", align_bytes=64)
+            nc.sync.dma_start(out=words[:].bitcast(I32), in_=tab_words[a].rearrange("p n t -> p (n t)").bitcast(I32))
+            table.append(words)
+            raw = ring.tile([P, PACK, H], F32, name="raw")
+            rows = w1[a * K_PASS : (a + 1) * K_PASS, :].rearrange("(p j) c -> p j c", j=PACK)
+            if a < PASSES - 1:
+                nc.sync.dma_start(out=raw[:], in_=rows)
+            else:
+                for half in range(2):
+                    cols = slice(half * H // 2, (half + 1) * H // 2)
+                    nc.sync.dma_start(out=raw[:, :, cols], in_=rows[:, :, cols])
+            w1_raw.append(raw)
+            if a == 0:
+                nc.sync.dma_start(places[:], offs2)
+
+        page_rows = page0.rearrange("(p t) c -> p t c", t=PACK)
+        wgs_rows = wgs.rearrange("(q t) j -> q t j", t=PACK)
+        page = [keep.tile([P, T2], F32, name=f"page{t}") for t in range(PACK)]
+        weights = [keep.tile([P, S], F32, name=f"weights{t}") for t in range(PACK)]
+
+        def load_weights(t, cols):
+            for q in (0, 2, 1, 3):
+                nc.sync.dma_start(out=weights[t][32 * q : 32 * q + 32, cols], in_=wgs_rows[:, t, cols])
+
+        nc.sync.dma_start(out=page[0][:], in_=page_rows[:, 0, :])
+        load_weights(0, slice(0, BANK))
+        wb_raw = keep.tile([P, PACK, N], F32, name="wb_raw")
+        nc.sync.dma_start(out=wb_raw[:], in_=wb.rearrange("(p j) c -> p j c", j=PACK))
+        load_weights(0, slice(BANK, S))
+
+        picked_scales = keep.tile([P, S], U8, name="picked_scales", align_bytes=64)
+        nc.vector.tensor_copy(out=picked_scales[:], in_=table_scales[:].indirect(picks[:]))
+
+        sums = [[psum.tile([P, BANK], F32, name="bank") for h in range(HALVES)] for t in range(PACK)]
+        for a in range(PASSES):
+            picked = keep.tile([P, S], U32, name=f"picked{a}", align_bytes=64)
+            nc.vector.tensor_copy(out=picked[:], in_=table[a][:].indirect(picks[:]))
+            grouped = ring.tile([P, PACK * H], BF16, name="grouped", align_bytes=64, bufs=2)
+            dealt = grouped[:].rearrange("p (t m j) -> p m j t", t=PACK, j=PACK)
+            source = w1_raw[a][:].rearrange("p j (m t) -> p m j t", t=PACK)
+            codes = keep.tile([P, H], U32, name=f"w1_codes{a}", align_bytes=64)
+            plane = keep.tile([P, H], U8, name=f"w1_plane{a}", align_bytes=64)
+            if a < PASSES - 1:
+                nc.scalar.copy(out=dealt, in_=source)
+                spans = [(0, H)]
+            else:
+                nc.scalar.copy(out=dealt[:, : P // 2], in_=source[:, : P // 2])
+                nc.vector.tensor_copy(out=dealt[:, P // 2 :], in_=source[:, P // 2 :])
+                spans = [(0, P), (P, 2 * P), (2 * P, H)]
+            for lo, hi in spans:
+                nc.vector.quantize_mx(
+                    out=codes[:, lo:hi].bitcast(FP8X4), scales=plane[:, lo:hi], in_=grouped[:, PACK * lo : PACK * hi]
+                )
+            for t in range(PACK):
+                for h in range(HALVES):
+                    rows = slice(t * P, (t + 1) * P)
+                    cols = slice(h * BANK, (h + 1) * BANK)
+                    nc.tensor.matmul_mx(
+                        out=sums[t][h][:],
+                        lhsT=codes[:, rows].bitcast(FP8X4),
+                        lhsT_scale=plane[:, rows],
+                        rhs=picked[:, cols].bitcast(FP8X4),
+                        rhs_scale=picked_scales[4 * a : P, cols],
+                        start=(a == 0),
+                        stop=(a == PASSES - 1),
+                    )
+
+        for t in range(1, PACK):
+            nc.sync.dma_start(out=page[t][:], in_=page_rows[:, t, :])
+            load_weights(t, slice(0, S))
+        wa_codes = keep.tile([P, 2 * N], U8, name="wa_codes", align_bytes=64)
+        nc.sync.dma_start(out=wa_codes[:].bitcast(I32), in_=wa_words[0].bitcast(I32))
+        appeal_cols = keep.tile([P, N // P], F32, name="appeal_cols")
+        with nc.allow_non_contiguous_dma(reason="one bias value for each partition"):
+            nc.sync.dma_start(out=appeal_cols[:], in_=appeal.rearrange("(b p) -> p b", p=P))
+
+        starts = [sum(CHUNKS[:c]) for c in range(len(CHUNKS))]
+        woven = [keep.tile([P, PACK * w], BF16, name=f"woven{c}", align_bytes=64) for c, w in enumerate(CHUNKS)]
+        out_rows = out_1.rearrange("(p t) c -> p t c", t=PACK)
+
+        def weave(t, c, lo, hi):
+            target = woven[c][:].rearrange("p (m t) -> p m t", t=PACK)[:, lo:hi]
+            source = page[t][:, starts[c] + lo : starts[c] + hi]
+            if c >= VECTOR_CHUNKS or t < PACK - 2:
+                nc.scalar.copy(out=target[:, :, t], in_=source)
+            elif t == PACK - 2:
+                nc.scalar.copy(out=target[:, :, t:], in_=source.unsqueeze(2).to_broadcast([P, hi - lo, 2]))
+            else:
+                nc.vector.tensor_copy(out=target[:, :, t], in_=source)
+
+        units = [(t, h) for t in range(PACK) for h in range(HALVES)]
+        states, factors = {}, {}
+        for t, h in units:
+            factor = keep.tile([P, BANK], F32, name=f"factor{t}{h}")
+            nc.scalar.activation(out=factor[:], in_=sums[t][h][:], func=IDENTITY, bias=1.0, scale=curve_cols[:, t : t + 1])
+            factors[t, h] = factor
+        wb_grouped = ring.tile([P, PACK * N], BF16, name="grouped", align_bytes=64, bufs=2)
+        nc.scalar.copy(
+            out=wb_grouped[:].rearrange("p (c i j) -> p c j i", i=PACK, j=PACK),
+            in_=wb_raw[:].rearrange("p j (c i) -> p c j i", i=PACK),
+        )
+
+        def make_state(t, h):
+            state = ring.tile([P, BANK], F32, name="state", tag="state", align_bytes=64)
+            nc.vector.tensor_tensor(out=state[:], in0=sums[t][h][:], in1=factors[t, h][:], op=MULT)
+            states[t, h] = state
+
+        def scatter(t, h):
+            nc.vector.tensor_tensor(
+                out=page[t][:].indirect(places[:, h * LIST_COLS : (h + 1) * LIST_COLS]),
+                in0=states[t, h][:],
+                in1=weights[t][:, h * BANK : (h + 1) * BANK],
+                op=MULT,
+            )
+
+        wb_plane = keep.tile([P, N], U8, name="wb_plane", align_bytes=64)
+        make_state(*units[0])
+        make_state(*units[1])
+        for i, (t, h) in enumerate(units):
+            scatter(t, h)
+            if i + 2 < len(units):
+                make_state(*units[i + 2])
+            if i == len(units) - 2:
+                wb_codes = ring.tile([P, N], U32, name="wb_codes", tag="state", align_bytes=64)
+                nc.vector.quantize_mx(out=wb_codes[:].bitcast(FP8X4), scales=wb_plane[:], in_=wb_grouped[:])
+            if h == HALVES - 1:
+                nc.sync.dma_start(out=out_rows[:, t, :], in_=page[t][:])
+                if t < PACK - 1:
+                    for c in range(len(CHUNKS)):
+                        weave(t, c, 0, CHUNKS[c])
+
+        page_codes = keep.tile([P, T2], U32, name="page_codes", align_bytes=64)
+        page_plane = keep.tile([P, T2], U8, name="page_plane", align_bytes=64)
+        words_out = out_2[0].rearrange("p m t -> p (m t)").bitcast(I32)
+        score_rows = out_0.rearrange("(b p) c -> p b c", p=P)
+
+        def quantize_page(c):
+            cols = slice(starts[c], starts[c] + CHUNKS[c])
+            nc.vector.quantize_mx(out=page_codes[:, cols].bitcast(FP8X4), scales=page_plane[:, cols], in_=woven[c][:])
+            nc.sync.dma_start(out=words_out[:, cols], in_=page_codes[:, cols].bitcast(I32))
+
+        def products(c, b0):
+            width = CHUNKS[c]
+            cols = slice(starts[c], starts[c] + width)
+            fit = psum.tile([P, BANK], F32, name="bank")
+            want = psum.tile([P, BANK], F32, name="bank")
+            for i in range(BANK // width):
+                b = b0 + i
+                nc.tensor.matmul_mx(
+                    out=fit[:, i * width : (i + 1) * width],
+                    lhsT=wa_codes[:, 2 * b * P : 2 * (b + 1) * P].bitcast(FP4X4),
+                    lhsT_scale=wa_plane[:, b * P : (b + 1) * P],
+                    rhs=page_codes[:, cols].bitcast(FP8X4),
+                    rhs_scale=page_plane[:, cols],
+                    start=True,
+                    stop=True,
+                )
+            for i in range(BANK // width):
+                b = b0 + i
+                nc.tensor.matmul_mx(
+                    out=want[:, i * width : (i + 1) * width],
+                    lhsT=wb_codes[:, b * P : (b + 1) * P].bitcast(FP8X4),
+                    lhsT_scale=wb_plane[:, b * P : (b + 1) * P],
+                    rhs=page_codes[:, cols].bitcast(FP8X4),
+                    rhs_scale=page_plane[:, cols],
+                    start=True,
+                    stop=True,
+                )
+            fit_copy = ring.tile([P, BANK], F32, name="fit_copy")
+            nc.scalar.copy(out=fit_copy[:], in_=fit[:])
+            score = ring.tile([P, BANK], F32, name="score", bufs=6)
+            nc.vector.tensor_tensor(out=score[:], in0=want[:], in1=fit_copy[:], op=MULT)
+            return score
+
+        def finish(index, c, b0, score):
+            width = CHUNKS[c]
+            count = BANK // width
+            for i in range(count):
+                part = score[:, i * width : (i + 1) * width]
+                bias = appeal_cols[:, b0 + i : b0 + i + 1]
+                if index % SCALAR_ADD_EVERY == SCALAR_ADD_EVERY - 2 and index > 4:
+                    nc.scalar.activation(out=part, in_=part, func=IDENTITY, bias=bias)
+                else:
+                    nc.vector.tensor_scalar(out=part, in0=part, scalar1=bias, scalar2=None, op0=ADD)
+            nc.sync.dma_start(
+                out=score_rows[:, b0 : b0 + count, starts[c] : starts[c] + width],
+                in_=score[:].rearrange("p (i w) -> p i w", i=count),
+            )
+
+        last = PACK - 1
+        weave(last, 0, 0, CHUNKS[0])
+        weave(last, 1, 0, CHUNKS[1])
+        quantize_page(0)
+        weave(last, 2, 0, CHUNKS[2])
+        quantize_page(1)
+        late_weaves = [(c, lo, lo + BANK // 2) for c in range(VECTOR_CHUNKS, len(CHUNKS)) for lo in (0, BANK // 2)]
+        score_units = [(c, b0) for c, width in enumerate(CHUNKS) for b0 in range(0, N // P, BANK // width)]
+        scores = []
+        for index, (c, b0) in enumerate(score_units):
+            if index % 2 == 0 and index // 2 < len(late_weaves):
+                weave(last, *late_weaves[index // 2])
+            if b0 == 0 and 2 <= c + 1 < len(CHUNKS) and c > 0:
+                quantize_page(c + 1)
+            scores.append(products(c, b0))
+            if index >= 1:
+                finish(index - 1, *score_units[index - 1], scores[index - 1])
+        finish(len(score_units) - 1, *score_units[-1], scores[-1])
+        for q in range(4):
+            nc.gpsimd.dma_start(
+                out=out_3[0, 4 * q : 4 * q + 4, :].bitcast(I32), in_=page_plane[32 * q : 32 * q + 4, :].bitcast(I32)
+            )

@@ -26,7 +26,7 @@ HALVES = S // BANK
 LIST_COLS = BANK // 16
 CHUNKS = [256, 256, 512, 512, 512]
 VECTOR_CHUNKS = 3
-SCALAR_ADD_EVERY = 4
+SCALAR_ADDS = range(9, 15)
 
 
 def tile_list_recipe_taste_store_kernel(
@@ -43,101 +43,105 @@ def tile_list_recipe_taste_store_kernel(
         places = keep.tile([P, S // 16], U16, name="places")
         nc.sync.dma_start(picks[:], offs)
 
-        table_scales = keep.tile([P, T], U8, name="table_scales", align_bytes=64)
-        nc.vector.memset(table_scales[:].bitcast(I32), 0)
-        for q in range(4):
-            nc.gpsimd.dma_start(
-                out=table_scales[32 * q : 32 * q + 4 * PASSES, :].bitcast(I32),
-                in_=tab_scales[:, 4 * q : 4 * q + 4, :].bitcast(I32),
-            )
-        curve_cols = keep.tile([P, PACK], F32, name="curve_cols")
-        nc.gpsimd.dma_start(out=curve_cols[:], in_=curve.rearrange("(p t) -> p t", t=PACK))
-        wa_plane = keep.tile([P, N], U8, name="wa_plane", align_bytes=64)
-        nc.vector.memset(wa_plane[:].bitcast(I32), 0)
-        for q in range(4):
-            nc.gpsimd.dma_start(
-                out=wa_plane[32 * q : 32 * q + 4, :].bitcast(I32),
-                in_=wa_scales[0, 4 * q : 4 * q + 4, :].bitcast(I32),
-            )
+        with tc.tile_pool(name="early", bufs=1) as early:
+            table_scales = early.tile([P, T], U8, name="table_scales", align_bytes=64)
+            nc.vector.memset(table_scales[:].bitcast(I32), 0)
 
-        table, w1_raw = [], []
-        for a in range(PASSES):
-            words = keep.tile([P, T], U32, name=f"table{a}", align_bytes=64)
-            nc.sync.dma_start(out=words[:].bitcast(I32), in_=tab_words[a].rearrange("p n t -> p (n t)").bitcast(I32))
-            table.append(words)
-            raw = ring.tile([P, PACK, H], F32, name="raw")
-            rows = w1[a * K_PASS : (a + 1) * K_PASS, :].rearrange("(p j) c -> p j c", j=PACK)
-            if a < PASSES - 1:
-                nc.sync.dma_start(out=raw[:], in_=rows)
-            else:
-                for half in range(2):
-                    cols = slice(half * H // 2, (half + 1) * H // 2)
-                    nc.sync.dma_start(out=raw[:, :, cols], in_=rows[:, :, cols])
-            w1_raw.append(raw)
-            if a == 0:
-                nc.sync.dma_start(places[:], offs2)
+            table, w1_raw = [], []
+            for a in range(PASSES):
+                words = early.tile([P, T], U32, name=f"table{a}", align_bytes=64)
+                nc.sync.dma_start(out=words[:].bitcast(I32), in_=tab_words[a].rearrange("p n t -> p (n t)").bitcast(I32))
+                table.append(words)
+                if a == 0:
+                    for q in range(4):
+                        nc.sync.dma_start(
+                            out=table_scales[32 * q : 32 * q + 4 * PASSES, :].bitcast(I32),
+                            in_=tab_scales[:, 4 * q : 4 * q + 4, :].bitcast(I32),
+                        )
+                raw = early.tile([P, PACK, H], F32, name=f"w1_raw{a}")
+                rows = w1[a * K_PASS : (a + 1) * K_PASS, :].rearrange("(p j) c -> p j c", j=PACK)
+                if a < PASSES - 1:
+                    nc.sync.dma_start(out=raw[:], in_=rows)
+                else:
+                    for half in range(2):
+                        cols = slice(half * H // 2, (half + 1) * H // 2)
+                        nc.sync.dma_start(out=raw[:, :, cols], in_=rows[:, :, cols])
+                w1_raw.append(raw)
+                if a == 1:
+                    nc.sync.dma_start(places[:], offs2)
+                    curve_cols = keep.tile([P, PACK], F32, name="curve_cols")
+                    nc.sync.dma_start(out=curve_cols[:], in_=curve.rearrange("(p t) -> p t", t=PACK))
 
-        page_rows = page0.rearrange("(p t) c -> p t c", t=PACK)
-        wgs_rows = wgs.rearrange("(q t) j -> q t j", t=PACK)
-        page = [keep.tile([P, T2], F32, name=f"page{t}") for t in range(PACK)]
-        weights = [keep.tile([P, S], F32, name=f"weights{t}") for t in range(PACK)]
+            page_rows = page0.rearrange("(p t) c -> p t c", t=PACK)
+            wgs_rows = wgs.rearrange("(q t) j -> q t j", t=PACK)
+            page = [keep.tile([P, T2], F32, name=f"page{t}") for t in range(PACK)]
+            weights = [keep.tile([P, S], F32, name=f"weights{t}") for t in range(PACK)]
 
-        def load_weights(t, cols):
-            for q in (0, 2, 1, 3):
-                nc.sync.dma_start(out=weights[t][32 * q : 32 * q + 32, cols], in_=wgs_rows[:, t, cols])
+            def load_weights(t, cols):
+                for q in (0, 2, 1, 3):
+                    nc.sync.dma_start(out=weights[t][32 * q : 32 * q + 32, cols], in_=wgs_rows[:, t, cols])
 
-        nc.sync.dma_start(out=page[0][:], in_=page_rows[:, 0, :])
-        load_weights(0, slice(0, BANK))
-        wb_raw = keep.tile([P, PACK, N], F32, name="wb_raw")
-        nc.sync.dma_start(out=wb_raw[:], in_=wb.rearrange("(p j) c -> p j c", j=PACK))
-        load_weights(0, slice(BANK, S))
+            wa_plane = keep.tile([P, N], U8, name="wa_plane", align_bytes=64)
+            nc.vector.memset(wa_plane[:].bitcast(I32), 0)
+            nc.sync.dma_start(out=page[0][:], in_=page_rows[:, 0, :])
+            for h in range(HALVES):
+                load_weights(0, slice(h * BANK, (h + 1) * BANK))
 
-        picked_scales = keep.tile([P, S], U8, name="picked_scales", align_bytes=64)
-        nc.vector.tensor_copy(out=picked_scales[:], in_=table_scales[:].indirect(picks[:]))
+            picked_scales = keep.tile([P, S], U8, name="picked_scales", align_bytes=64)
+            nc.vector.tensor_copy(out=picked_scales[:], in_=table_scales[:].indirect(picks[:]))
 
-        sums = [[psum.tile([P, BANK], F32, name="bank") for h in range(HALVES)] for t in range(PACK)]
-        for a in range(PASSES):
-            picked = keep.tile([P, S], U32, name=f"picked{a}", align_bytes=64)
-            nc.vector.tensor_copy(out=picked[:], in_=table[a][:].indirect(picks[:]))
-            grouped = ring.tile([P, PACK * H], BF16, name="grouped", align_bytes=64, bufs=2)
-            dealt = grouped[:].rearrange("p (t m j) -> p m j t", t=PACK, j=PACK)
-            source = w1_raw[a][:].rearrange("p j (m t) -> p m j t", t=PACK)
-            codes = keep.tile([P, H], U32, name=f"w1_codes{a}", align_bytes=64)
-            plane = keep.tile([P, H], U8, name=f"w1_plane{a}", align_bytes=64)
-            if a < PASSES - 1:
-                nc.scalar.copy(out=dealt, in_=source)
-                spans = [(0, H)]
-            else:
-                nc.scalar.copy(out=dealt[:, : P // 2], in_=source[:, : P // 2])
-                nc.vector.tensor_copy(out=dealt[:, P // 2 :], in_=source[:, P // 2 :])
-                spans = [(0, P), (P, 2 * P), (2 * P, H)]
-            for lo, hi in spans:
-                nc.vector.quantize_mx(
-                    out=codes[:, lo:hi].bitcast(FP8X4), scales=plane[:, lo:hi], in_=grouped[:, PACK * lo : PACK * hi]
-                )
-            for t in range(PACK):
-                for h in range(HALVES):
-                    rows = slice(t * P, (t + 1) * P)
-                    cols = slice(h * BANK, (h + 1) * BANK)
-                    nc.tensor.matmul_mx(
-                        out=sums[t][h][:],
-                        lhsT=codes[:, rows].bitcast(FP8X4),
-                        lhsT_scale=plane[:, rows],
-                        rhs=picked[:, cols].bitcast(FP8X4),
-                        rhs_scale=picked_scales[4 * a : P, cols],
-                        start=(a == 0),
-                        stop=(a == PASSES - 1),
+            sums = [[psum.tile([P, BANK], F32, name="bank") for h in range(HALVES)] for t in range(PACK)]
+            for a in range(PASSES):
+                picked = keep.tile([P, S], U32, name=f"picked{a}", align_bytes=64)
+                nc.vector.tensor_copy(out=picked[:], in_=table[a][:].indirect(picks[:]))
+                grouped = ring.tile([P, PACK * H], BF16, name="grouped", align_bytes=64, bufs=2)
+                dealt = grouped[:].rearrange("p (t m j) -> p m j t", t=PACK, j=PACK)
+                source = w1_raw[a][:].rearrange("p j (m t) -> p m j t", t=PACK)
+                codes = keep.tile([P, H], U32, name=f"w1_codes{a}", align_bytes=64)
+                plane = keep.tile([P, H], U8, name=f"w1_plane{a}", align_bytes=64)
+                if a < PASSES - 1:
+                    nc.scalar.copy(out=dealt, in_=source)
+                    spans = [(0, H)]
+                else:
+                    nc.scalar.copy(out=dealt[:, : P // 2], in_=source[:, : P // 2])
+                    nc.vector.tensor_copy(out=dealt[:, P // 2 :], in_=source[:, P // 2 :])
+                    spans = [(0, P), (P, 2 * P), (2 * P, H)]
+                for lo, hi in spans:
+                    nc.vector.quantize_mx(
+                        out=codes[:, lo:hi].bitcast(FP8X4), scales=plane[:, lo:hi], in_=grouped[:, PACK * lo : PACK * hi]
                     )
+                for t in range(PACK):
+                    for h in range(HALVES):
+                        rows = slice(t * P, (t + 1) * P)
+                        cols = slice(h * BANK, (h + 1) * BANK)
+                        nc.tensor.matmul_mx(
+                            out=sums[t][h][:],
+                            lhsT=codes[:, rows].bitcast(FP8X4),
+                            lhsT_scale=plane[:, rows],
+                            rhs=picked[:, cols].bitcast(FP8X4),
+                            rhs_scale=picked_scales[4 * a : P, cols],
+                            start=(a == 0),
+                            stop=(a == PASSES - 1),
+                        )
 
         for t in range(1, PACK):
             nc.sync.dma_start(out=page[t][:], in_=page_rows[:, t, :])
             load_weights(t, slice(0, S))
+            if t == 1:
+                wb_raw = keep.tile([P, PACK, N], F32, name="wb_raw")
+                nc.sync.dma_start(out=wb_raw[:], in_=wb.rearrange("(p j) c -> p j c", j=PACK))
         wa_codes = keep.tile([P, 2 * N], U8, name="wa_codes", align_bytes=64)
         nc.sync.dma_start(out=wa_codes[:].bitcast(I32), in_=wa_words[0].bitcast(I32))
+        for q in range(4):
+            nc.sync.dma_start(
+                out=wa_plane[32 * q : 32 * q + 4, :].bitcast(I32),
+                in_=wa_scales[0, 4 * q : 4 * q + 4, :].bitcast(I32),
+            )
         appeal_cols = keep.tile([P, N // P], F32, name="appeal_cols")
         with nc.allow_non_contiguous_dma(reason="one bias value for each partition"):
             nc.sync.dma_start(out=appeal_cols[:], in_=appeal.rearrange("(b p) -> p b", p=P))
 
+        late = ctx.enter_context(tc.tile_pool(name="late", bufs=1))
         starts = [sum(CHUNKS[:c]) for c in range(len(CHUNKS))]
         woven = [keep.tile([P, PACK * w], BF16, name=f"woven{c}", align_bytes=64) for c, w in enumerate(CHUNKS)]
         out_rows = out_1.rearrange("(p t) c -> p t c", t=PACK)
@@ -177,7 +181,6 @@ def tile_list_recipe_taste_store_kernel(
                 op=MULT,
             )
 
-        wb_plane = keep.tile([P, N], U8, name="wb_plane", align_bytes=64)
         make_state(*units[0])
         make_state(*units[1])
         for i, (t, h) in enumerate(units):
@@ -185,6 +188,7 @@ def tile_list_recipe_taste_store_kernel(
             if i + 2 < len(units):
                 make_state(*units[i + 2])
             if i == len(units) - 2:
+                wb_plane = ring.tile([P, N], U8, name="wb_plane", tag="state", align_bytes=64)
                 wb_codes = ring.tile([P, N], U32, name="wb_codes", tag="state", align_bytes=64)
                 nc.vector.quantize_mx(out=wb_codes[:].bitcast(FP8X4), scales=wb_plane[:], in_=wb_grouped[:])
             if h == HALVES - 1:
@@ -230,9 +234,9 @@ def tile_list_recipe_taste_store_kernel(
                     start=True,
                     stop=True,
                 )
-            fit_copy = ring.tile([P, BANK], F32, name="fit_copy")
+            fit_copy = late.tile([P, BANK], F32, name="fit_copy", bufs=6)
             nc.scalar.copy(out=fit_copy[:], in_=fit[:])
-            score = ring.tile([P, BANK], F32, name="score", bufs=6)
+            score = late.tile([P, BANK], F32, name=f"score{c}_{b0}")
             nc.vector.tensor_tensor(out=score[:], in0=want[:], in1=fit_copy[:], op=MULT)
             return score
 
@@ -242,7 +246,7 @@ def tile_list_recipe_taste_store_kernel(
             for i in range(count):
                 part = score[:, i * width : (i + 1) * width]
                 bias = appeal_cols[:, b0 + i : b0 + i + 1]
-                if index % SCALAR_ADD_EVERY == SCALAR_ADD_EVERY - 2 and index > 4:
+                if index in SCALAR_ADDS:
                     nc.scalar.activation(out=part, in_=part, func=IDENTITY, bias=bias)
                 else:
                     nc.vector.tensor_scalar(out=part, in0=part, scalar1=bias, scalar2=None, op0=ADD)
@@ -255,8 +259,9 @@ def tile_list_recipe_taste_store_kernel(
         weave(last, 0, 0, CHUNKS[0])
         weave(last, 1, 0, CHUNKS[1])
         quantize_page(0)
-        weave(last, 2, 0, CHUNKS[2])
         quantize_page(1)
+        weave(last, 2, 0, BANK // 2)
+        weave(last, 2, BANK // 2, BANK)
         late_weaves = [(c, lo, lo + BANK // 2) for c in range(VECTOR_CHUNKS, len(CHUNKS)) for lo in (0, BANK // 2)]
         score_units = [(c, b0) for c, width in enumerate(CHUNKS) for b0 in range(0, N // P, BANK // width)]
         scores = []
@@ -270,6 +275,6 @@ def tile_list_recipe_taste_store_kernel(
                 finish(index - 1, *score_units[index - 1], scores[index - 1])
         finish(len(score_units) - 1, *score_units[-1], scores[-1])
         for q in range(4):
-            nc.gpsimd.dma_start(
+            nc.sync.dma_start(
                 out=out_3[0, 4 * q : 4 * q + 4, :].bitcast(I32), in_=page_plane[32 * q : 32 * q + 4, :].bitcast(I32)
             )

@@ -37,6 +37,7 @@ def tile_list_recipe_taste_store_kernel(
     with ExitStack() as ctx:
         keep = ctx.enter_context(tc.tile_pool(name="keep", bufs=1))
         ring = ctx.enter_context(tc.tile_pool(name="ring", bufs=3))
+        slots = ctx.enter_context(tc.tile_pool(name="slots", bufs=1))
         psum = ctx.enter_context(tc.psum_pool(name="psum", bufs=8))
 
         picks = keep.tile([P, S // 16], U16, name="picks")
@@ -48,6 +49,13 @@ def tile_list_recipe_taste_store_kernel(
             nc.vector.memset(table_scales[:].bitcast(I32), 0)
 
             table, w1_raw = [], []
+
+            def load_w1(a):
+                raw = early.tile([P, PACK, H], F32, name=f"w1_raw{a}")
+                rows = w1[a * K_PASS : (a + 1) * K_PASS, :].rearrange("(p j) c -> p j c", j=PACK)
+                nc.sync.dma_start(out=raw[:], in_=rows)
+                w1_raw.append(raw)
+
             for a in range(PASSES):
                 words = early.tile([P, T], U32, name=f"table{a}", align_bytes=64)
                 nc.sync.dma_start(out=words[:].bitcast(I32), in_=tab_words[a].rearrange("p n t -> p (n t)").bitcast(I32))
@@ -58,16 +66,10 @@ def tile_list_recipe_taste_store_kernel(
                             out=table_scales[32 * q : 32 * q + 4 * PASSES, :].bitcast(I32),
                             in_=tab_scales[:, 4 * q : 4 * q + 4, :].bitcast(I32),
                         )
-                raw = early.tile([P, PACK, H], F32, name=f"w1_raw{a}")
-                rows = w1[a * K_PASS : (a + 1) * K_PASS, :].rearrange("(p j) c -> p j c", j=PACK)
                 if a < PASSES - 1:
-                    nc.sync.dma_start(out=raw[:], in_=rows)
-                else:
-                    for half in range(2):
-                        cols = slice(half * H // 2, (half + 1) * H // 2)
-                        nc.sync.dma_start(out=raw[:, :, cols], in_=rows[:, :, cols])
-                w1_raw.append(raw)
-                if a == 1:
+                    load_w1(a)
+                if a == PASSES - 2:
+                    load_w1(PASSES - 1)
                     nc.sync.dma_start(places[:], offs2)
                     curve_cols = keep.tile([P, PACK], F32, name="curve_cols")
                     nc.sync.dma_start(out=curve_cols[:], in_=curve.rearrange("(p t) -> p t", t=PACK))
@@ -92,24 +94,23 @@ def tile_list_recipe_taste_store_kernel(
 
             sums = [[psum.tile([P, BANK], F32, name="bank") for h in range(HALVES)] for t in range(PACK)]
             for a in range(PASSES):
-                picked = keep.tile([P, S], U32, name=f"picked{a}", align_bytes=64)
-                nc.vector.tensor_copy(out=picked[:], in_=table[a][:].indirect(picks[:]))
                 grouped = ring.tile([P, PACK * H], BF16, name="grouped", align_bytes=64, bufs=2)
-                dealt = grouped[:].rearrange("p (t m j) -> p m j t", t=PACK, j=PACK)
-                source = w1_raw[a][:].rearrange("p j (m t) -> p m j t", t=PACK)
                 codes = keep.tile([P, H], U32, name=f"w1_codes{a}", align_bytes=64)
                 plane = keep.tile([P, H], U8, name=f"w1_plane{a}", align_bytes=64)
+                nc.scalar.copy(
+                    out=grouped[:].rearrange("p (t m j) -> p m j t", t=PACK, j=PACK),
+                    in_=w1_raw[a][:].rearrange("p j (m t) -> p m j t", t=PACK),
+                )
+                picked = keep.tile([P, S], U32, name=f"picked{a}", align_bytes=64)
                 if a < PASSES - 1:
-                    nc.scalar.copy(out=dealt, in_=source)
-                    spans = [(0, H)]
-                else:
-                    nc.scalar.copy(out=dealt[:, : P // 2], in_=source[:, : P // 2])
-                    nc.vector.tensor_copy(out=dealt[:, P // 2 :], in_=source[:, P // 2 :])
-                    spans = [(0, P), (P, 2 * P), (2 * P, H)]
-                for lo, hi in spans:
-                    nc.vector.quantize_mx(
-                        out=codes[:, lo:hi].bitcast(FP8X4), scales=plane[:, lo:hi], in_=grouped[:, PACK * lo : PACK * hi]
-                    )
+                    nc.vector.tensor_copy(out=picked[:], in_=table[a][:].indirect(picks[:]))
+                nc.vector.quantize_mx(out=codes[:].bitcast(FP8X4), scales=plane[:], in_=grouped[:])
+                if a == PASSES - 1:
+                    for h in range(HALVES):
+                        nc.vector.tensor_copy(
+                            out=picked[:, h * BANK : (h + 1) * BANK],
+                            in_=table[a][:].indirect(picks[:, h * LIST_COLS : (h + 1) * LIST_COLS]),
+                        )
                 for t in range(PACK):
                     for h in range(HALVES):
                         rows = slice(t * P, (t + 1) * P)
@@ -157,40 +158,44 @@ def tile_list_recipe_taste_store_kernel(
                 nc.vector.tensor_copy(out=target[:, :, t], in_=source)
 
         units = [(t, h) for t in range(PACK) for h in range(HALVES)]
-        states, factors = {}, {}
-        for t, h in units:
-            factor = keep.tile([P, BANK], F32, name=f"factor{t}{h}")
+        factors, plain, values = {}, {}, {}
+        for i, (t, h) in enumerate(units):
+            factor = keep.tile([P, BANK], F32, name=f"factor{i}")
             nc.scalar.activation(out=factor[:], in_=sums[t][h][:], func=IDENTITY, bias=1.0, scale=curve_cols[:, t : t + 1])
-            factors[t, h] = factor
-        wb_grouped = ring.tile([P, PACK * N], BF16, name="grouped", align_bytes=64, bufs=2)
-        nc.scalar.copy(
+            factors[i] = factor
+            if i > 0:
+                copy = late.tile([P, BANK], F32, name=f"plain{i}")
+                nc.scalar.copy(out=copy[:], in_=sums[t][h][:])
+                plain[i] = copy
+
+        for i, (t, h) in enumerate(units):
+            weight = weights[t][:, h * BANK : (h + 1) * BANK]
+            state = slots.tile([P, BANK], F32, name=f"state{i}", offset=4 * BANK * (i % 2), align_bytes=64)
+            value = slots.tile([P, BANK], F32, name=f"value{i}", offset=4 * BANK * (len(units) + 1 - i), align_bytes=64)
+            if i == 0:
+                nc.vector.tensor_tensor(out=state[:], in0=sums[t][h][:], in1=factors[i][:], op=MULT)
+                nc.vector.tensor_tensor(out=value[:], in0=state[:], in1=weight, op=MULT)
+            else:
+                nc.gpsimd.tensor_tensor(out=state[:], in0=plain[i][:], in1=factors[i][:], op=MULT)
+                nc.gpsimd.tensor_tensor(out=value[:], in0=state[:], in1=weight, op=MULT)
+            values[i] = value
+        wb_grouped = slots.tile([P, PACK * N], BF16, name="wb_grouped", offset=0, align_bytes=64)
+        nc.gpsimd.tensor_scalar(
             out=wb_grouped[:].rearrange("p (c i j) -> p c j i", i=PACK, j=PACK),
-            in_=wb_raw[:].rearrange("p j (c i) -> p c j i", i=PACK),
+            in0=wb_raw[:].rearrange("p j (c i) -> p c j i", i=PACK),
+            scalar1=1.0,
+            scalar2=0.0,
+            op0=MULT,
+            op1=ADD,
         )
 
-        def make_state(t, h):
-            state = ring.tile([P, BANK], F32, name="state", tag="state", align_bytes=64)
-            nc.vector.tensor_tensor(out=state[:], in0=sums[t][h][:], in1=factors[t, h][:], op=MULT)
-            states[t, h] = state
-
         def scatter(t, h):
-            nc.vector.tensor_tensor(
-                out=page[t][:].indirect(places[:, h * LIST_COLS : (h + 1) * LIST_COLS]),
-                in0=states[t, h][:],
-                in1=weights[t][:, h * BANK : (h + 1) * BANK],
-                op=MULT,
+            nc.vector.tensor_copy(
+                out=page[t][:].indirect(places[:, h * LIST_COLS : (h + 1) * LIST_COLS]), in_=values[HALVES * t + h][:]
             )
 
-        make_state(*units[0])
-        make_state(*units[1])
         for i, (t, h) in enumerate(units):
             scatter(t, h)
-            if i + 2 < len(units):
-                make_state(*units[i + 2])
-            if i == len(units) - 2:
-                wb_plane = ring.tile([P, N], U8, name="wb_plane", tag="state", align_bytes=64)
-                wb_codes = ring.tile([P, N], U32, name="wb_codes", tag="state", align_bytes=64)
-                nc.vector.quantize_mx(out=wb_codes[:].bitcast(FP8X4), scales=wb_plane[:], in_=wb_grouped[:])
             if h == HALVES - 1:
                 nc.sync.dma_start(out=out_rows[:, t, :], in_=page[t][:])
                 if t < PACK - 1:
@@ -259,6 +264,9 @@ def tile_list_recipe_taste_store_kernel(
         weave(last, 0, 0, CHUNKS[0])
         weave(last, 1, 0, CHUNKS[1])
         quantize_page(0)
+        wb_plane = keep.tile([P, N], U8, name="wb_plane", align_bytes=64)
+        wb_codes = slots.tile([P, N], U32, name="wb_codes", offset=8 * BANK, align_bytes=64)
+        nc.vector.quantize_mx(out=wb_codes[:].bitcast(FP8X4), scales=wb_plane[:], in_=wb_grouped[:])
         quantize_page(1)
         weave(last, 2, 0, BANK // 2)
         weave(last, 2, BANK // 2, BANK)

@@ -24,9 +24,10 @@ PASSES = K // K_PASS
 BANK = 512
 HALVES = S // BANK
 LIST_COLS = BANK // 16
-CHUNKS = [256, 256, 512, 512, 512]
-VECTOR_CHUNKS = 3
-SCALAR_ADDS = range(9, 15)
+CHUNKS = [512, 512, 512, 512]
+VECTOR_CHUNKS = 2
+ADD_CYCLE = 4
+SPLIT_TILES = 2
 
 
 def tile_list_recipe_taste_store_kernel(
@@ -126,9 +127,9 @@ def tile_list_recipe_taste_store_kernel(
                         )
 
         for t in range(1, PACK):
-            nc.sync.dma_start(out=page[t][:], in_=page_rows[:, t, :])
             load_weights(t, slice(0, S))
-            if t == 1:
+            nc.sync.dma_start(out=page[t][:], in_=page_rows[:, t, :])
+            if t == 2:
                 wb_raw = keep.tile([P, PACK, N], F32, name="wb_raw")
                 nc.sync.dma_start(out=wb_raw[:], in_=wb.rearrange("(p j) c -> p j c", j=PACK))
         wa_codes = keep.tile([P, 2 * N], U8, name="wa_codes", align_bytes=64)
@@ -157,28 +158,28 @@ def tile_list_recipe_taste_store_kernel(
             else:
                 nc.vector.tensor_copy(out=target[:, :, t], in_=source)
 
-        units = [(t, h) for t in range(PACK) for h in range(HALVES)]
-        factors, plain, values = {}, {}, {}
-        for i, (t, h) in enumerate(units):
-            factor = keep.tile([P, BANK], F32, name=f"factor{i}")
-            nc.scalar.activation(out=factor[:], in_=sums[t][h][:], func=IDENTITY, bias=1.0, scale=curve_cols[:, t : t + 1])
-            factors[i] = factor
-            if i > 0:
-                copy = late.tile([P, BANK], F32, name=f"plain{i}")
-                nc.scalar.copy(out=copy[:], in_=sums[t][h][:])
-                plain[i] = copy
+        factors = [keep.tile([P, S], F32, name=f"factor{t}") for t in range(PACK)]
+        plain = [late.tile([P, S], F32, name=f"plain{t}") for t in range(PACK)]
+        for t in range(PACK):
+            for h in range(HALVES):
+                cols = slice(h * BANK, (h + 1) * BANK)
+                nc.scalar.activation(
+                    out=factors[t][:, cols], in_=sums[t][h][:], func=IDENTITY, bias=1.0, scale=curve_cols[:, t : t + 1]
+                )
+                if (t, h) != (0, 0):
+                    nc.scalar.copy(out=plain[t][:, cols], in_=sums[t][h][:])
 
-        for i, (t, h) in enumerate(units):
-            weight = weights[t][:, h * BANK : (h + 1) * BANK]
-            state = slots.tile([P, BANK], F32, name=f"state{i}", offset=4 * BANK * (i % 2), align_bytes=64)
-            value = slots.tile([P, BANK], F32, name=f"value{i}", offset=4 * BANK * (len(units) + 1 - i), align_bytes=64)
+        pieces = [(t, h * BANK, (h + 1) * BANK) for t in range(SPLIT_TILES) for h in range(HALVES)]
+        pieces = pieces + [(t, 0, S) for t in range(SPLIT_TILES, PACK)]
+        values = [slots.tile([P, S], F32, name=f"value{t}", offset=4 * S * (PACK + 1 - t), align_bytes=64) for t in range(PACK)]
+        for i, (t, lo, hi) in enumerate(pieces):
+            state = slots.tile([P, hi - lo], F32, name=f"state{i}", offset=4 * S * (i == 0), align_bytes=64)
             if i == 0:
-                nc.vector.tensor_tensor(out=state[:], in0=sums[t][h][:], in1=factors[i][:], op=MULT)
-                nc.vector.tensor_tensor(out=value[:], in0=state[:], in1=weight, op=MULT)
+                nc.vector.tensor_tensor(out=state[:], in0=sums[0][0][:], in1=factors[0][:, lo:hi], op=MULT)
+                nc.vector.tensor_tensor(out=values[0][:, lo:hi], in0=state[:], in1=weights[0][:, lo:hi], op=MULT)
             else:
-                nc.gpsimd.tensor_tensor(out=state[:], in0=plain[i][:], in1=factors[i][:], op=MULT)
-                nc.gpsimd.tensor_tensor(out=value[:], in0=state[:], in1=weight, op=MULT)
-            values[i] = value
+                nc.gpsimd.tensor_tensor(out=state[:], in0=plain[t][:, lo:hi], in1=factors[t][:, lo:hi], op=MULT)
+                nc.gpsimd.tensor_tensor(out=values[t][:, lo:hi], in0=state[:], in1=weights[t][:, lo:hi], op=MULT)
         wb_grouped = slots.tile([P, PACK * N], BF16, name="wb_grouped", offset=0, align_bytes=64)
         nc.gpsimd.tensor_scalar(
             out=wb_grouped[:].rearrange("p (c i j) -> p c j i", i=PACK, j=PACK),
@@ -189,14 +190,9 @@ def tile_list_recipe_taste_store_kernel(
             op1=ADD,
         )
 
-        def scatter(t, h):
-            nc.vector.tensor_copy(
-                out=page[t][:].indirect(places[:, h * LIST_COLS : (h + 1) * LIST_COLS]), in_=values[HALVES * t + h][:]
-            )
-
-        for i, (t, h) in enumerate(units):
-            scatter(t, h)
-            if h == HALVES - 1:
+        for t, lo, hi in pieces:
+            nc.vector.tensor_copy(out=page[t][:].indirect(places[:, lo // 16 : hi // 16]), in_=values[t][:, lo:hi])
+            if hi == S:
                 nc.sync.dma_start(out=out_rows[:, t, :], in_=page[t][:])
                 if t < PACK - 1:
                     for c in range(len(CHUNKS)):
@@ -251,33 +247,33 @@ def tile_list_recipe_taste_store_kernel(
             for i in range(count):
                 part = score[:, i * width : (i + 1) * width]
                 bias = appeal_cols[:, b0 + i : b0 + i + 1]
-                if index in SCALAR_ADDS:
+                turn = (15 - index) % ADD_CYCLE
+                if index == 15:
+                    nc.vector.tensor_scalar(out=part, in0=part, scalar1=bias, scalar2=None, op0=ADD)
+                elif turn == 0:
                     nc.scalar.activation(out=part, in_=part, func=IDENTITY, bias=bias)
                 else:
-                    nc.vector.tensor_scalar(out=part, in0=part, scalar1=bias, scalar2=None, op0=ADD)
+                    nc.gpsimd.tensor_scalar(out=part, in0=part, scalar1=1.0, scalar2=bias, op0=MULT, op1=ADD)
             nc.sync.dma_start(
                 out=score_rows[:, b0 : b0 + count, starts[c] : starts[c] + width],
                 in_=score[:].rearrange("p (i w) -> p i w", i=count),
             )
 
         last = PACK - 1
+        for c in range(VECTOR_CHUNKS, len(CHUNKS)):
+            weave(last, c, 0, CHUNKS[c])
         weave(last, 0, 0, CHUNKS[0])
-        weave(last, 1, 0, CHUNKS[1])
-        quantize_page(0)
         wb_plane = keep.tile([P, N], U8, name="wb_plane", align_bytes=64)
-        wb_codes = slots.tile([P, N], U32, name="wb_codes", offset=8 * BANK, align_bytes=64)
+        wb_codes = slots.tile([P, N], U32, name="wb_codes", offset=8 * S, align_bytes=64)
         nc.vector.quantize_mx(out=wb_codes[:].bitcast(FP8X4), scales=wb_plane[:], in_=wb_grouped[:])
-        quantize_page(1)
-        weave(last, 2, 0, BANK // 2)
-        weave(last, 2, BANK // 2, BANK)
-        late_weaves = [(c, lo, lo + BANK // 2) for c in range(VECTOR_CHUNKS, len(CHUNKS)) for lo in (0, BANK // 2)]
-        score_units = [(c, b0) for c, width in enumerate(CHUNKS) for b0 in range(0, N // P, BANK // width)]
+        quantize_page(0)
+        weave(last, 1, 0, CHUNKS[1])
+        order = (0, 2, 1, 3)
+        for c in order[1:]:
+            quantize_page(c)
+        score_units = [(c, b0) for c in order for b0 in range(N // P)]
         scores = []
         for index, (c, b0) in enumerate(score_units):
-            if index % 2 == 0 and index // 2 < len(late_weaves):
-                weave(last, *late_weaves[index // 2])
-            if b0 == 0 and 2 <= c + 1 < len(CHUNKS) and c > 0:
-                quantize_page(c + 1)
             scores.append(products(c, b0))
             if index >= 1:
                 finish(index - 1, *score_units[index - 1], scores[index - 1])

@@ -23,10 +23,14 @@ K_PASS = P * PACK
 PASSES = K // K_PASS
 BANK = 512
 HALVES = S // BANK
-LIST_COLS = BANK // 16
-CHUNKS = [512, 512, 512, 512]
-VECTOR_CHUNKS = 2
-ADD_CYCLE = 4
+CHUNKS = T2 // BANK
+BLOCKS = N // P
+UNITS = CHUNKS * BLOCKS
+KIB = 1024
+VECTOR_COLS = 1024
+W1_VECTOR = 84
+SCALAR_ADDS = (3, 7, 11, 14)
+ADD_LAG = 2
 SPLIT_TILES = 2
 
 
@@ -37,95 +41,59 @@ def tile_list_recipe_taste_store_kernel(
     nc = tc.nc
     with ExitStack() as ctx:
         keep = ctx.enter_context(tc.tile_pool(name="keep", bufs=1))
-        ring = ctx.enter_context(tc.tile_pool(name="ring", bufs=3))
+        arena = ctx.enter_context(tc.tile_pool(name="arena", bufs=1))
         slots = ctx.enter_context(tc.tile_pool(name="slots", bufs=1))
         psum = ctx.enter_context(tc.psum_pool(name="psum", bufs=8))
+
+        def place(shape, dtype, name, kib):
+            return arena.tile(shape, dtype, name=name, offset=kib * KIB, align_bytes=64)
 
         picks = keep.tile([P, S // 16], U16, name="picks")
         places = keep.tile([P, S // 16], U16, name="places")
         nc.sync.dma_start(picks[:], offs)
 
-        with tc.tile_pool(name="early", bufs=1) as early:
-            table_scales = early.tile([P, T], U8, name="table_scales", align_bytes=64)
-            nc.vector.memset(table_scales[:].bitcast(I32), 0)
+        table_scales = place([P, T], U8, "table_scales", 72)
+        nc.vector.memset(table_scales[:].bitcast(I32), 0)
+        table = [place([P, T], U32, f"table{a}", 16 * a) for a in range(PASSES)]
+        w1_raw = [place([P, PACK, H], F32, f"w1_raw{a}", 48 + 8 * a) for a in range(PASSES)]
 
-            table, w1_raw = [], []
+        def load_table(a):
+            words = tab_words[a].rearrange("p n t -> p (n t)").bitcast(I32)
+            nc.sync.dma_start(out=table[a][:].bitcast(I32), in_=words)
 
-            def load_w1(a):
-                raw = early.tile([P, PACK, H], F32, name=f"w1_raw{a}")
-                rows = w1[a * K_PASS : (a + 1) * K_PASS, :].rearrange("(p j) c -> p j c", j=PACK)
-                nc.sync.dma_start(out=raw[:], in_=rows)
-                w1_raw.append(raw)
+        def load_w1(a):
+            rows = w1[a * K_PASS : (a + 1) * K_PASS, :].rearrange("(p j) c -> p j c", j=PACK)
+            nc.sync.dma_start(out=w1_raw[a][:], in_=rows)
 
-            for a in range(PASSES):
-                words = early.tile([P, T], U32, name=f"table{a}", align_bytes=64)
-                nc.sync.dma_start(out=words[:].bitcast(I32), in_=tab_words[a].rearrange("p n t -> p (n t)").bitcast(I32))
-                table.append(words)
-                if a == 0:
-                    for q in range(4):
-                        nc.sync.dma_start(
-                            out=table_scales[32 * q : 32 * q + 4 * PASSES, :].bitcast(I32),
-                            in_=tab_scales[:, 4 * q : 4 * q + 4, :].bitcast(I32),
-                        )
-                if a < PASSES - 1:
-                    load_w1(a)
-                if a == PASSES - 2:
-                    load_w1(PASSES - 1)
-                    nc.sync.dma_start(places[:], offs2)
-                    curve_cols = keep.tile([P, PACK], F32, name="curve_cols")
-                    nc.sync.dma_start(out=curve_cols[:], in_=curve.rearrange("(p t) -> p t", t=PACK))
+        load_table(0)
+        for q in range(4):
+            nc.sync.dma_start(
+                out=table_scales[32 * q : 32 * q + 4 * PASSES, :].bitcast(I32),
+                in_=tab_scales[:, 4 * q : 4 * q + 4, :].bitcast(I32),
+            )
+        load_w1(0)
+        load_table(1)
+        load_w1(1)
+        load_w1(2)
+        nc.sync.dma_start(places[:], offs2)
+        curve_cols = keep.tile([P, PACK], F32, name="curve_cols")
+        nc.sync.dma_start(out=curve_cols[:], in_=curve.rearrange("(p t) -> p t", t=PACK))
+        load_table(2)
 
-            page_rows = page0.rearrange("(p t) c -> p t c", t=PACK)
-            wgs_rows = wgs.rearrange("(q t) j -> q t j", t=PACK)
-            page = [keep.tile([P, T2], F32, name=f"page{t}") for t in range(PACK)]
-            weights = [keep.tile([P, S], F32, name=f"weights{t}") for t in range(PACK)]
+        page_rows = page0.rearrange("(p t) c -> p t c", t=PACK)
+        wgs_rows = wgs.rearrange("(q t) j -> q t j", t=PACK)
+        page = [keep.tile([P, T2], F32, name=f"page{t}") for t in range(PACK)]
+        weights = [keep.tile([P, S], F32, name=f"weights{t}") for t in range(PACK)]
 
-            def load_weights(t, cols):
-                for q in (0, 2, 1, 3):
-                    nc.sync.dma_start(out=weights[t][32 * q : 32 * q + 32, cols], in_=wgs_rows[:, t, cols])
+        def load_weights(t, cols):
+            for q in (0, 2, 1, 3):
+                nc.sync.dma_start(out=weights[t][32 * q : 32 * q + 32, cols], in_=wgs_rows[:, t, cols])
 
-            wa_plane = keep.tile([P, N], U8, name="wa_plane", align_bytes=64)
-            nc.vector.memset(wa_plane[:].bitcast(I32), 0)
-            nc.sync.dma_start(out=page[0][:], in_=page_rows[:, 0, :])
-            for h in range(HALVES):
-                load_weights(0, slice(h * BANK, (h + 1) * BANK))
-
-            picked_scales = keep.tile([P, S], U8, name="picked_scales", align_bytes=64)
-            nc.vector.tensor_copy(out=picked_scales[:], in_=table_scales[:].indirect(picks[:]))
-
-            sums = [[psum.tile([P, BANK], F32, name="bank") for h in range(HALVES)] for t in range(PACK)]
-            for a in range(PASSES):
-                grouped = ring.tile([P, PACK * H], BF16, name="grouped", align_bytes=64, bufs=2)
-                codes = keep.tile([P, H], U32, name=f"w1_codes{a}", align_bytes=64)
-                plane = keep.tile([P, H], U8, name=f"w1_plane{a}", align_bytes=64)
-                nc.scalar.copy(
-                    out=grouped[:].rearrange("p (t m j) -> p m j t", t=PACK, j=PACK),
-                    in_=w1_raw[a][:].rearrange("p j (m t) -> p m j t", t=PACK),
-                )
-                picked = keep.tile([P, S], U32, name=f"picked{a}", align_bytes=64)
-                if a < PASSES - 1:
-                    nc.vector.tensor_copy(out=picked[:], in_=table[a][:].indirect(picks[:]))
-                nc.vector.quantize_mx(out=codes[:].bitcast(FP8X4), scales=plane[:], in_=grouped[:])
-                if a == PASSES - 1:
-                    for h in range(HALVES):
-                        nc.vector.tensor_copy(
-                            out=picked[:, h * BANK : (h + 1) * BANK],
-                            in_=table[a][:].indirect(picks[:, h * LIST_COLS : (h + 1) * LIST_COLS]),
-                        )
-                for t in range(PACK):
-                    for h in range(HALVES):
-                        rows = slice(t * P, (t + 1) * P)
-                        cols = slice(h * BANK, (h + 1) * BANK)
-                        nc.tensor.matmul_mx(
-                            out=sums[t][h][:],
-                            lhsT=codes[:, rows].bitcast(FP8X4),
-                            lhsT_scale=plane[:, rows],
-                            rhs=picked[:, cols].bitcast(FP8X4),
-                            rhs_scale=picked_scales[4 * a : P, cols],
-                            start=(a == 0),
-                            stop=(a == PASSES - 1),
-                        )
-
+        wa_plane = keep.tile([P, N], U8, name="wa_plane", align_bytes=64)
+        nc.vector.memset(wa_plane[:].bitcast(I32), 0)
+        nc.sync.dma_start(out=page[0][:], in_=page_rows[:, 0, :])
+        for h in range(HALVES):
+            load_weights(0, slice(h * BANK, (h + 1) * BANK))
         for t in range(1, PACK):
             load_weights(t, slice(0, S))
             nc.sync.dma_start(out=page[t][:], in_=page_rows[:, t, :])
@@ -139,19 +107,73 @@ def tile_list_recipe_taste_store_kernel(
                 out=wa_plane[32 * q : 32 * q + 4, :].bitcast(I32),
                 in_=wa_scales[0, 4 * q : 4 * q + 4, :].bitcast(I32),
             )
-        appeal_cols = keep.tile([P, N // P], F32, name="appeal_cols")
+        appeal_cols = keep.tile([P, BLOCKS], F32, name="appeal_cols")
         with nc.allow_non_contiguous_dma(reason="one bias value for each partition"):
             nc.sync.dma_start(out=appeal_cols[:], in_=appeal.rearrange("(b p) -> p b", p=P))
 
-        late = ctx.enter_context(tc.tile_pool(name="late", bufs=1))
-        starts = [sum(CHUNKS[:c]) for c in range(len(CHUNKS))]
-        woven = [keep.tile([P, PACK * w], BF16, name=f"woven{c}", align_bytes=64) for c, w in enumerate(CHUNKS)]
+        picked_scales = keep.tile([P, S], U8, name="picked_scales", align_bytes=64)
+        nc.vector.tensor_copy(out=picked_scales[:], in_=table_scales[:].indirect(picks[:]))
+
+        sums = [[psum.tile([P, BANK], F32, name="bank") for h in range(HALVES)] for t in range(PACK)]
+        grouped = [place([P, PACK * H], BF16, f"grouped{a}", kib) for a, kib in enumerate((0, 16, 20))]
+        picked = [place([P, S], U32, f"picked{a}", kib) for a, kib in enumerate((76, 80, 21))]
+
+        def round_w1(a):
+            dealt = grouped[a][:].rearrange("p (t m j) -> p m j t", t=PACK, j=PACK)
+            loaded = w1_raw[a][:].rearrange("p j (m t) -> p m j t", t=PACK)
+            nc.scalar.copy(out=dealt[:, W1_VECTOR:], in_=loaded[:, W1_VECTOR:])
+            nc.vector.tensor_copy(out=dealt[:, :W1_VECTOR], in_=loaded[:, :W1_VECTOR])
+
+        def quantize_w1(a, first, count, codes):
+            plane = keep.tile([P, count * P], U8, name=f"w1_plane{a}_{first}", align_bytes=64)
+            columns = slice(first * K_PASS, (first + count) * K_PASS)
+            nc.vector.quantize_mx(out=codes[:].bitcast(FP8X4), scales=plane[:], in_=grouped[a][:, columns])
+            return plane
+
+        def multiply(a, first, count, codes, plane):
+            for t in range(count):
+                for h in range(HALVES):
+                    rows = slice(t * P, (t + 1) * P)
+                    cols = slice(h * BANK, (h + 1) * BANK)
+                    nc.tensor.matmul_mx(
+                        out=sums[first + t][h][:],
+                        lhsT=codes[:, rows].bitcast(FP8X4),
+                        lhsT_scale=plane[:, rows],
+                        rhs=picked[a][:, cols].bitcast(FP8X4),
+                        rhs_scale=picked_scales[4 * a : P, cols],
+                        start=(a == 0),
+                        stop=(a == PASSES - 1),
+                    )
+
+        for a in range(PASSES - 1):
+            nc.vector.tensor_copy(out=picked[a][:], in_=table[a][:].indirect(picks[:]))
+            round_w1(a)
+            if a == 0:
+                codes = keep.tile([P, H], U32, name="w1_codes0", align_bytes=64)
+                multiply(0, 0, PACK, codes, quantize_w1(0, 0, PACK, codes))
+        round_w1(2)
+        held_codes = place([P, H], U32, "held_codes", 64)
+        multiply(1, 0, PACK, held_codes, quantize_w1(1, 0, PACK, held_codes))
+        last_codes = keep.tile([P, H], U32, name="w1_codes2", align_bytes=64)
+        last_plane = quantize_w1(2, 0, PACK, last_codes)
+        for h in range(HALVES):
+            cols = slice(h * BANK, (h + 1) * BANK)
+            nc.vector.tensor_copy(
+                out=picked[2][:, cols], in_=table[2][:].indirect(picks[:, cols.start // 16 : cols.stop // 16])
+            )
+        multiply(2, 0, PACK, last_codes, last_plane)
+
+        woven = [keep.tile([P, PACK * BANK], BF16, name=f"woven{c}", align_bytes=64) for c in range(CHUNKS)]
         out_rows = out_1.rearrange("(p t) c -> p t c", t=PACK)
+        parts = []
+        for c in range(CHUNKS):
+            cut = min(max(VECTOR_COLS - c * BANK, 0), BANK)
+            parts = parts + [(c, lo, hi) for lo, hi in ((0, cut), (cut, BANK)) if hi > lo]
 
         def weave(t, c, lo, hi):
             target = woven[c][:].rearrange("p (m t) -> p m t", t=PACK)[:, lo:hi]
-            source = page[t][:, starts[c] + lo : starts[c] + hi]
-            if c >= VECTOR_CHUNKS or t < PACK - 2:
+            source = page[t][:, c * BANK + lo : c * BANK + hi]
+            if c * BANK + lo >= VECTOR_COLS or t < PACK - 2:
                 nc.scalar.copy(out=target[:, :, t], in_=source)
             elif t == PACK - 2:
                 nc.scalar.copy(out=target[:, :, t:], in_=source.unsqueeze(2).to_broadcast([P, hi - lo, 2]))
@@ -159,7 +181,7 @@ def tile_list_recipe_taste_store_kernel(
                 nc.vector.tensor_copy(out=target[:, :, t], in_=source)
 
         factors = [keep.tile([P, S], F32, name=f"factor{t}") for t in range(PACK)]
-        plain = [late.tile([P, S], F32, name=f"plain{t}") for t in range(PACK)]
+        plain = [place([P, S], F32, f"plain{t}", 48 + 4 * t) for t in range(PACK)]
         for t in range(PACK):
             for h in range(HALVES):
                 cols = slice(h * BANK, (h + 1) * BANK)
@@ -194,9 +216,12 @@ def tile_list_recipe_taste_store_kernel(
             nc.vector.tensor_copy(out=page[t][:].indirect(places[:, lo // 16 : hi // 16]), in_=values[t][:, lo:hi])
             if hi == S:
                 nc.sync.dma_start(out=out_rows[:, t, :], in_=page[t][:])
-                if t < PACK - 1:
-                    for c in range(len(CHUNKS)):
-                        weave(t, c, 0, CHUNKS[c])
+                if t < PACK - 2:
+                    for c in range(CHUNKS):
+                        weave(t, c, 0, BANK)
+                if t == PACK - 2:
+                    for part in parts:
+                        weave(t, *part)
 
         page_codes = keep.tile([P, T2], U32, name="page_codes", align_bytes=64)
         page_plane = keep.tile([P, T2], U8, name="page_plane", align_bytes=64)
@@ -204,80 +229,80 @@ def tile_list_recipe_taste_store_kernel(
         score_rows = out_0.rearrange("(b p) c -> p b c", p=P)
 
         def quantize_page(c):
-            cols = slice(starts[c], starts[c] + CHUNKS[c])
+            cols = slice(c * BANK, (c + 1) * BANK)
             nc.vector.quantize_mx(out=page_codes[:, cols].bitcast(FP8X4), scales=page_plane[:, cols], in_=woven[c][:])
             nc.sync.dma_start(out=words_out[:, cols], in_=page_codes[:, cols].bitcast(I32))
 
-        def products(c, b0):
-            width = CHUNKS[c]
-            cols = slice(starts[c], starts[c] + width)
+        def fit_slot(index):
+            return 16 + 2 * index if index < 8 else 48 + 2 * index
+
+        def products(index, c, b):
+            cols = slice(c * BANK, (c + 1) * BANK)
             fit = psum.tile([P, BANK], F32, name="bank")
             want = psum.tile([P, BANK], F32, name="bank")
-            for i in range(BANK // width):
-                b = b0 + i
-                nc.tensor.matmul_mx(
-                    out=fit[:, i * width : (i + 1) * width],
-                    lhsT=wa_codes[:, 2 * b * P : 2 * (b + 1) * P].bitcast(FP4X4),
-                    lhsT_scale=wa_plane[:, b * P : (b + 1) * P],
-                    rhs=page_codes[:, cols].bitcast(FP8X4),
-                    rhs_scale=page_plane[:, cols],
-                    start=True,
-                    stop=True,
-                )
-            for i in range(BANK // width):
-                b = b0 + i
-                nc.tensor.matmul_mx(
-                    out=want[:, i * width : (i + 1) * width],
-                    lhsT=wb_codes[:, b * P : (b + 1) * P].bitcast(FP8X4),
-                    lhsT_scale=wb_plane[:, b * P : (b + 1) * P],
-                    rhs=page_codes[:, cols].bitcast(FP8X4),
-                    rhs_scale=page_plane[:, cols],
-                    start=True,
-                    stop=True,
-                )
-            fit_copy = late.tile([P, BANK], F32, name="fit_copy", bufs=6)
+            nc.tensor.matmul_mx(
+                out=fit[:],
+                lhsT=wa_codes[:, 2 * b * P : 2 * (b + 1) * P].bitcast(FP4X4),
+                lhsT_scale=wa_plane[:, b * P : (b + 1) * P],
+                rhs=page_codes[:, cols].bitcast(FP8X4),
+                rhs_scale=page_plane[:, cols],
+                start=True,
+                stop=True,
+            )
+            nc.tensor.matmul_mx(
+                out=want[:],
+                lhsT=wb_codes[:, b * P : (b + 1) * P].bitcast(FP8X4),
+                lhsT_scale=wb_plane[:, b * P : (b + 1) * P],
+                rhs=page_codes[:, cols].bitcast(FP8X4),
+                rhs_scale=page_plane[:, cols],
+                start=True,
+                stop=True,
+            )
+            fit_copy = place([P, BANK], F32, f"fit_copy{index}", fit_slot(index))
             nc.scalar.copy(out=fit_copy[:], in_=fit[:])
-            score = late.tile([P, BANK], F32, name=f"score{c}_{b0}")
+            score = place([P, BANK], F32, f"score{index}", 2 * index if index < 8 else 16 + 2 * index)
             nc.vector.tensor_tensor(out=score[:], in0=want[:], in1=fit_copy[:], op=MULT)
             return score
 
-        def finish(index, c, b0, score):
-            width = CHUNKS[c]
-            count = BANK // width
-            for i in range(count):
-                part = score[:, i * width : (i + 1) * width]
-                bias = appeal_cols[:, b0 + i : b0 + i + 1]
-                turn = (15 - index) % ADD_CYCLE
-                if index == 15:
-                    nc.vector.tensor_scalar(out=part, in0=part, scalar1=bias, scalar2=None, op0=ADD)
-                elif turn == 0:
-                    nc.scalar.activation(out=part, in_=part, func=IDENTITY, bias=bias)
-                else:
-                    nc.gpsimd.tensor_scalar(out=part, in0=part, scalar1=1.0, scalar2=bias, op0=MULT, op1=ADD)
-            nc.sync.dma_start(
-                out=score_rows[:, b0 : b0 + count, starts[c] : starts[c] + width],
-                in_=score[:].rearrange("p (i w) -> p i w", i=count),
-            )
+        def finish(index, c, b, score):
+            bias = appeal_cols[:, b : b + 1]
+            if index == UNITS - 1:
+                nc.vector.tensor_scalar(out=score[:], in0=score[:], scalar1=bias, scalar2=None, op0=ADD)
+            elif index == UNITS - 2:
+                nc.scalar.activation(out=score[:], in_=score[:], func=IDENTITY, bias=bias)
+            elif index in SCALAR_ADDS:
+                biased = place([P, BANK], F32, f"biased{index}", fit_slot(index + ADD_LAG))
+                nc.scalar.activation(out=biased[:], in_=score[:], func=IDENTITY, bias=bias)
+                score = biased
+            else:
+                nc.gpsimd.tensor_scalar(out=score[:], in0=score[:], scalar1=1.0, scalar2=bias, op0=MULT, op1=ADD)
+            nc.sync.dma_start(out=score_rows[:, b, c * BANK : (c + 1) * BANK], in_=score[:])
 
         last = PACK - 1
-        for c in range(VECTOR_CHUNKS, len(CHUNKS)):
-            weave(last, c, 0, CHUNKS[c])
-        weave(last, 0, 0, CHUNKS[0])
+        for c, lo, hi in parts:
+            if c * BANK + lo >= VECTOR_COLS:
+                weave(last, c, lo, hi)
+        weave(last, *parts[0])
         wb_plane = keep.tile([P, N], U8, name="wb_plane", align_bytes=64)
         wb_codes = slots.tile([P, N], U32, name="wb_codes", offset=8 * S, align_bytes=64)
         nc.vector.quantize_mx(out=wb_codes[:].bitcast(FP8X4), scales=wb_plane[:], in_=wb_grouped[:])
         quantize_page(0)
-        weave(last, 1, 0, CHUNKS[1])
+        for c, lo, hi in parts[1:]:
+            if c * BANK + lo < VECTOR_COLS:
+                weave(last, c, lo, hi)
         order = (0, 2, 1, 3)
         for c in order[1:]:
             quantize_page(c)
-        score_units = [(c, b0) for c in order for b0 in range(N // P)]
+        score_units = [(c, b) for c in order for b in range(BLOCKS)]
         scores = []
-        for index, (c, b0) in enumerate(score_units):
-            scores.append(products(c, b0))
-            if index >= 1:
+        for index, (c, b) in enumerate(score_units):
+            scores.append(products(index, c, b))
+            if index >= 1 and index - 1 not in SCALAR_ADDS:
                 finish(index - 1, *score_units[index - 1], scores[index - 1])
-        finish(len(score_units) - 1, *score_units[-1], scores[-1])
+            if index - ADD_LAG in SCALAR_ADDS:
+                finish(index - ADD_LAG, *score_units[index - ADD_LAG], scores[index - ADD_LAG])
+        for index in (UNITS - 2, UNITS - 1):
+            finish(index, *score_units[index], scores[index])
         for q in range(4):
             nc.sync.dma_start(
                 out=out_3[0, 4 * q : 4 * q + 4, :].bitcast(I32), in_=page_plane[32 * q : 32 * q + 4, :].bitcast(I32)

@@ -43,14 +43,12 @@ def tile_list_recipe_taste_store_kernel(
         keep = ctx.enter_context(tc.tile_pool(name="keep", bufs=1))
         arena = ctx.enter_context(tc.tile_pool(name="arena", bufs=1))
         slots = ctx.enter_context(tc.tile_pool(name="slots", bufs=1))
-        psum = ctx.enter_context(tc.psum_pool(name="psum", bufs=8))
 
         def place(shape, dtype, name, kib):
             return arena.tile(shape, dtype, name=name, offset=kib * KIB, align_bytes=64)
 
         picks = keep.tile([P, S // 16], U16, name="picks")
         places = keep.tile([P, S // 16], U16, name="places")
-        nc.sync.dma_start(picks[:], offs)
 
         table_scales = place([P, T], U8, "table_scales", 72)
         nc.vector.memset(table_scales[:].bitcast(I32), 0)
@@ -66,8 +64,9 @@ def tile_list_recipe_taste_store_kernel(
             nc.sync.dma_start(out=w1_raw[a][:], in_=rows)
 
         load_table(0)
+        nc.sync.dma_start(picks[:], offs)
         for q in range(4):
-            nc.sync.dma_start(
+            nc.gpsimd.dma_start(
                 out=table_scales[32 * q : 32 * q + 4 * PASSES, :].bitcast(I32),
                 in_=tab_scales[:, 4 * q : 4 * q + 4, :].bitcast(I32),
             )
@@ -75,10 +74,10 @@ def tile_list_recipe_taste_store_kernel(
         load_table(1)
         load_w1(1)
         load_w1(2)
-        nc.sync.dma_start(places[:], offs2)
+        load_table(2)
         curve_cols = keep.tile([P, PACK], F32, name="curve_cols")
         nc.sync.dma_start(out=curve_cols[:], in_=curve.rearrange("(p t) -> p t", t=PACK))
-        load_table(2)
+        nc.sync.dma_start(places[:], offs2)
 
         page_rows = page0.rearrange("(p t) c -> p t c", t=PACK)
         wgs_rows = wgs.rearrange("(q t) j -> q t j", t=PACK)
@@ -111,97 +110,104 @@ def tile_list_recipe_taste_store_kernel(
         with nc.allow_non_contiguous_dma(reason="one bias value for each partition"):
             nc.sync.dma_start(out=appeal_cols[:], in_=appeal.rearrange("(b p) -> p b", p=P))
 
-        picked_scales = keep.tile([P, S], U8, name="picked_scales", align_bytes=64)
-        nc.vector.tensor_copy(out=picked_scales[:], in_=table_scales[:].indirect(picks[:]))
+        picked_scales = place([P, S], U8, "picked_scales", 26)
+        with tc.psum_pool(name="first_banks", bufs=4) as first_banks:
+            sums = [[first_banks.tile([P, BANK], F32, name="sum") for h in range(HALVES)] for t in range(PACK)]
+            grouped = [place([P, PACK * H], BF16, f"grouped{a}", kib) for a, kib in enumerate((0, 4, 20))]
+            picked = [place([P, S], U32, f"picked{a}", kib) for a, kib in enumerate((76, 80, 21))]
 
-        sums = [[psum.tile([P, BANK], F32, name="bank") for h in range(HALVES)] for t in range(PACK)]
-        grouped = [place([P, PACK * H], BF16, f"grouped{a}", kib) for a, kib in enumerate((0, 16, 20))]
-        picked = [place([P, S], U32, f"picked{a}", kib) for a, kib in enumerate((76, 80, 21))]
+            def round_w1(a):
+                dealt = grouped[a][:].rearrange("p (t m j) -> p m j t", t=PACK, j=PACK)
+                loaded = w1_raw[a][:].rearrange("p j (m t) -> p m j t", t=PACK)
+                share = W1_VECTOR if a == PASSES - 1 else 0
+                nc.scalar.copy(out=dealt[:, share:], in_=loaded[:, share:])
+                if share:
+                    nc.vector.tensor_copy(out=dealt[:, :share], in_=loaded[:, :share])
 
-        def round_w1(a):
-            dealt = grouped[a][:].rearrange("p (t m j) -> p m j t", t=PACK, j=PACK)
-            loaded = w1_raw[a][:].rearrange("p j (m t) -> p m j t", t=PACK)
-            nc.scalar.copy(out=dealt[:, W1_VECTOR:], in_=loaded[:, W1_VECTOR:])
-            nc.vector.tensor_copy(out=dealt[:, :W1_VECTOR], in_=loaded[:, :W1_VECTOR])
+            def quantize_w1(a, codes):
+                plane = keep.tile([P, H], U8, name=f"w1_plane{a}", align_bytes=64)
+                nc.vector.quantize_mx(out=codes[:].bitcast(FP8X4), scales=plane[:], in_=grouped[a][:])
+                return codes, plane
 
-        def quantize_w1(a, first, count, codes):
-            plane = keep.tile([P, count * P], U8, name=f"w1_plane{a}_{first}", align_bytes=64)
-            columns = slice(first * K_PASS, (first + count) * K_PASS)
-            nc.vector.quantize_mx(out=codes[:].bitcast(FP8X4), scales=plane[:], in_=grouped[a][:, columns])
-            return plane
+            def multiply(a, t, h):
+                codes, plane = stationary[a]
+                rows = slice(t * P, (t + 1) * P)
+                cols = slice(h * BANK, (h + 1) * BANK)
+                nc.tensor.matmul_mx(
+                    out=sums[t][h][:],
+                    lhsT=codes[:, rows].bitcast(FP8X4),
+                    lhsT_scale=plane[:, rows],
+                    rhs=picked[a][:, cols].bitcast(FP8X4),
+                    rhs_scale=picked_scales[4 * a : P, cols],
+                    start=(a == 0),
+                    stop=(a == PASSES - 1),
+                )
 
-        def multiply(a, first, count, codes, plane):
-            for t in range(count):
-                for h in range(HALVES):
-                    rows = slice(t * P, (t + 1) * P)
-                    cols = slice(h * BANK, (h + 1) * BANK)
-                    nc.tensor.matmul_mx(
-                        out=sums[first + t][h][:],
-                        lhsT=codes[:, rows].bitcast(FP8X4),
-                        lhsT_scale=plane[:, rows],
-                        rhs=picked[a][:, cols].bitcast(FP8X4),
-                        rhs_scale=picked_scales[4 * a : P, cols],
-                        start=(a == 0),
-                        stop=(a == PASSES - 1),
-                    )
-
-        for a in range(PASSES - 1):
-            nc.vector.tensor_copy(out=picked[a][:], in_=table[a][:].indirect(picks[:]))
-            round_w1(a)
-            if a == 0:
-                codes = keep.tile([P, H], U32, name="w1_codes0", align_bytes=64)
-                multiply(0, 0, PACK, codes, quantize_w1(0, 0, PACK, codes))
-        round_w1(2)
-        held_codes = place([P, H], U32, "held_codes", 64)
-        multiply(1, 0, PACK, held_codes, quantize_w1(1, 0, PACK, held_codes))
-        last_codes = keep.tile([P, H], U32, name="w1_codes2", align_bytes=64)
-        last_plane = quantize_w1(2, 0, PACK, last_codes)
-        for h in range(HALVES):
-            cols = slice(h * BANK, (h + 1) * BANK)
-            nc.vector.tensor_copy(
-                out=picked[2][:, cols], in_=table[2][:].indirect(picks[:, cols.start // 16 : cols.stop // 16])
-            )
-        multiply(2, 0, PACK, last_codes, last_plane)
-
-        woven = [keep.tile([P, PACK * BANK], BF16, name=f"woven{c}", align_bytes=64) for c in range(CHUNKS)]
-        out_rows = out_1.rearrange("(p t) c -> p t c", t=PACK)
-        parts = []
-        for c in range(CHUNKS):
-            cut = min(max(VECTOR_COLS - c * BANK, 0), BANK)
-            parts = parts + [(c, lo, hi) for lo, hi in ((0, cut), (cut, BANK)) if hi > lo]
-
-        def weave(t, c, lo, hi):
-            target = woven[c][:].rearrange("p (m t) -> p m t", t=PACK)[:, lo:hi]
-            source = page[t][:, c * BANK + lo : c * BANK + hi]
-            if c * BANK + lo >= VECTOR_COLS or t < PACK - 2:
-                nc.scalar.copy(out=target[:, :, t], in_=source)
-            elif t == PACK - 2:
-                nc.scalar.copy(out=target[:, :, t:], in_=source.unsqueeze(2).to_broadcast([P, hi - lo, 2]))
-            else:
-                nc.vector.tensor_copy(out=target[:, :, t], in_=source)
-
-        factors = [keep.tile([P, S], F32, name=f"factor{t}") for t in range(PACK)]
-        plain = [place([P, S], F32, f"plain{t}", 48 + 4 * t) for t in range(PACK)]
-        for t in range(PACK):
+            stationary = []
+            for a in range(PASSES - 1):
+                nc.vector.tensor_copy(out=picked[a][:], in_=table[a][:].indirect(picks[:]))
+                round_w1(a)
+                if a == 0:
+                    stationary.append(quantize_w1(0, keep.tile([P, H], U32, name="w1_codes0", align_bytes=64)))
+            nc.vector.tensor_copy(out=picked_scales[:], in_=table_scales[:].indirect(picks[:]))
+            round_w1(2)
+            stationary.append(quantize_w1(1, place([P, H], U32, "held_codes", 64)))
+            stationary.append(quantize_w1(2, keep.tile([P, H], U32, name="w1_codes2", align_bytes=64)))
+            early_sums = [(t, h) for t in range(PACK // 2) for h in range(HALVES)]
+            for a in range(PASSES - 1):
+                for t, h in early_sums:
+                    multiply(a, t, h)
             for h in range(HALVES):
                 cols = slice(h * BANK, (h + 1) * BANK)
-                nc.scalar.activation(
-                    out=factors[t][:, cols], in_=sums[t][h][:], func=IDENTITY, bias=1.0, scale=curve_cols[:, t : t + 1]
+                nc.vector.tensor_copy(
+                    out=picked[2][:, cols], in_=table[2][:].indirect(picks[:, cols.start // 16 : cols.stop // 16])
                 )
-                if (t, h) != (0, 0):
-                    nc.scalar.copy(out=plain[t][:, cols], in_=sums[t][h][:])
+            for t, h in early_sums:
+                multiply(PASSES - 1, t, h)
 
-        pieces = [(t, h * BANK, (h + 1) * BANK) for t in range(SPLIT_TILES) for h in range(HALVES)]
-        pieces = pieces + [(t, 0, S) for t in range(SPLIT_TILES, PACK)]
-        values = [slots.tile([P, S], F32, name=f"value{t}", offset=4 * S * (PACK + 1 - t), align_bytes=64) for t in range(PACK)]
-        for i, (t, lo, hi) in enumerate(pieces):
-            state = slots.tile([P, hi - lo], F32, name=f"state{i}", offset=4 * S * (i == 0), align_bytes=64)
-            if i == 0:
-                nc.vector.tensor_tensor(out=state[:], in0=sums[0][0][:], in1=factors[0][:, lo:hi], op=MULT)
-                nc.vector.tensor_tensor(out=values[0][:, lo:hi], in0=state[:], in1=weights[0][:, lo:hi], op=MULT)
-            else:
-                nc.gpsimd.tensor_tensor(out=state[:], in0=plain[t][:, lo:hi], in1=factors[t][:, lo:hi], op=MULT)
-                nc.gpsimd.tensor_tensor(out=values[t][:, lo:hi], in0=state[:], in1=weights[t][:, lo:hi], op=MULT)
+            woven = [place([P, PACK * BANK], BF16, f"woven{c}", kib) for c, kib in enumerate((74, 78, 82, 19))]
+            out_rows = out_1.rearrange("(p t) c -> p t c", t=PACK)
+            parts = []
+            for c in range(CHUNKS):
+                cut = min(max(VECTOR_COLS - c * BANK, 0), BANK)
+                parts = parts + [(c, lo, hi) for lo, hi in ((0, cut), (cut, BANK)) if hi > lo]
+
+            def weave(t, c, lo, hi):
+                target = woven[c][:].rearrange("p (m t) -> p m t", t=PACK)[:, lo:hi]
+                source = page[t][:, c * BANK + lo : c * BANK + hi]
+                if c * BANK + lo >= VECTOR_COLS or t < PACK - 2:
+                    nc.scalar.copy(out=target[:, :, t], in_=source)
+                elif t == PACK - 2:
+                    nc.scalar.copy(out=target[:, :, t:], in_=source.unsqueeze(2).to_broadcast([P, hi - lo, 2]))
+                else:
+                    nc.vector.tensor_copy(out=target[:, :, t], in_=source)
+
+            factors = [keep.tile([P, S], F32, name=f"factor{t}") for t in range(PACK)]
+            plain = [place([P, S], F32, f"plain{t}", 48 + 4 * t) for t in range(PACK)]
+            for t in range(PACK):
+                for h in range(HALVES):
+                    cols = slice(h * BANK, (h + 1) * BANK)
+                    if (t, h) not in early_sums:
+                        for a in range(PASSES):
+                            multiply(a, t, h)
+                    nc.scalar.activation(
+                        out=factors[t][:, cols], in_=sums[t][h][:], func=IDENTITY, bias=1.0, scale=curve_cols[:, t : t + 1]
+                    )
+                    if (t, h) != (0, 0):
+                        nc.scalar.copy(out=plain[t][:, cols], in_=sums[t][h][:])
+
+            pieces = [(t, h * BANK, (h + 1) * BANK) for t in range(SPLIT_TILES) for h in range(HALVES)]
+            pieces = pieces + [(t, 0, S) for t in range(SPLIT_TILES, PACK)]
+            values = [slots.tile([P, S], F32, name=f"value{t}", offset=4 * S * (PACK + 1 - t), align_bytes=64) for t in range(PACK)]
+            for i, (t, lo, hi) in enumerate(pieces):
+                state = slots.tile([P, hi - lo], F32, name=f"state{i}", offset=4 * S * (i == 0), align_bytes=64)
+                if i == 0:
+                    nc.vector.tensor_tensor(out=state[:], in0=sums[0][0][:], in1=factors[0][:, lo:hi], op=MULT)
+                    nc.vector.tensor_tensor(out=values[0][:, lo:hi], in0=state[:], in1=weights[0][:, lo:hi], op=MULT)
+                else:
+                    nc.gpsimd.tensor_tensor(out=state[:], in0=plain[t][:, lo:hi], in1=factors[t][:, lo:hi], op=MULT)
+                    nc.gpsimd.tensor_tensor(out=values[t][:, lo:hi], in0=state[:], in1=weights[t][:, lo:hi], op=MULT)
+        psum = ctx.enter_context(tc.psum_pool(name="psum", bufs=8))
         wb_grouped = slots.tile([P, PACK * N], BF16, name="wb_grouped", offset=0, align_bytes=64)
         nc.gpsimd.tensor_scalar(
             out=wb_grouped[:].rearrange("p (c i j) -> p c j i", i=PACK, j=PACK),
@@ -234,7 +240,7 @@ def tile_list_recipe_taste_store_kernel(
             nc.sync.dma_start(out=words_out[:, cols], in_=page_codes[:, cols].bitcast(I32))
 
         def fit_slot(index):
-            return 16 + 2 * index if index < 8 else 48 + 2 * index
+            return 86 + 2 * index
 
         def products(index, c, b):
             cols = slice(c * BANK, (c + 1) * BANK)

@@ -77,7 +77,6 @@ def tile_list_recipe_taste_store_kernel(
         load_table(2)
         curve_cols = keep.tile([P, PACK], F32, name="curve_cols")
         nc.sync.dma_start(out=curve_cols[:], in_=curve.rearrange("(p t) -> p t", t=PACK))
-        nc.sync.dma_start(places[:], offs2)
 
         page_rows = page0.rearrange("(p t) c -> p t c", t=PACK)
         wgs_rows = wgs.rearrange("(q t) j -> q t j", t=PACK)
@@ -91,8 +90,9 @@ def tile_list_recipe_taste_store_kernel(
         wa_plane = keep.tile([P, N], U8, name="wa_plane", align_bytes=64)
         nc.vector.memset(wa_plane[:].bitcast(I32), 0)
         nc.sync.dma_start(out=page[0][:], in_=page_rows[:, 0, :])
-        for h in range(HALVES):
-            load_weights(0, slice(h * BANK, (h + 1) * BANK))
+        load_weights(0, slice(0, BANK))
+        nc.sync.dma_start(places[:], offs2)
+        load_weights(0, slice(BANK, S))
         for t in range(1, PACK):
             load_weights(t, slice(0, S))
             nc.sync.dma_start(out=page[t][:], in_=page_rows[:, t, :])

@@ -1,6 +1,7 @@
 from contextlib import ExitStack
 
 import concourse.mybir as mybir
+from concourse.masks import make_identity
 
 K, T, S, H, T2, N = 1536, 4096, 1024, 512, 2048, 512
 FLOPS = 2 * K * H * S + 2 * 2 * H * N * T2
@@ -29,8 +30,9 @@ UNITS = CHUNKS * BLOCKS
 KIB = 1024
 VECTOR_COLS = 1024
 W1_VECTOR = 84
-SCALAR_ADDS = (3, 7, 11, 14)
+SCALAR_ADDS = (4, 9, 14)
 ADD_LAG = 2
+EARLY_SUMS = 4
 SPLIT_TILES = 2
 
 
@@ -71,6 +73,10 @@ def tile_list_recipe_taste_store_kernel(
                 in_=tab_scales[:, 4 * q : 4 * q + 4, :].bitcast(I32),
             )
         load_w1(0)
+        wgs_rows = wgs.rearrange("(q t) j -> q t j", t=PACK)
+        first_rows = keep.tile([P, BANK], F32, name="first_rows")
+        nc.vector.memset(first_rows[:], 0.0)
+        nc.sync.dma_start(out=first_rows[0:P:PACK, :], in_=wgs_rows[:, 0, 0:BANK])
         load_table(1)
         load_w1(1)
         load_w1(2)
@@ -79,7 +85,6 @@ def tile_list_recipe_taste_store_kernel(
         nc.sync.dma_start(out=curve_cols[:], in_=curve.rearrange("(p t) -> p t", t=PACK))
 
         page_rows = page0.rearrange("(p t) c -> p t c", t=PACK)
-        wgs_rows = wgs.rearrange("(q t) j -> q t j", t=PACK)
         page = [keep.tile([P, T2], F32, name=f"page{t}") for t in range(PACK)]
         weights = [keep.tile([P, S], F32, name=f"weights{t}") for t in range(PACK)]
 
@@ -90,15 +95,14 @@ def tile_list_recipe_taste_store_kernel(
         wa_plane = keep.tile([P, N], U8, name="wa_plane", align_bytes=64)
         nc.vector.memset(wa_plane[:].bitcast(I32), 0)
         nc.sync.dma_start(out=page[0][:], in_=page_rows[:, 0, :])
-        load_weights(0, slice(0, BANK))
         nc.sync.dma_start(places[:], offs2)
         load_weights(0, slice(BANK, S))
         for t in range(1, PACK):
             load_weights(t, slice(0, S))
-            nc.sync.dma_start(out=page[t][:], in_=page_rows[:, t, :])
-            if t == 2:
+            if t == PACK - 1:
                 wb_raw = keep.tile([P, PACK, N], F32, name="wb_raw")
                 nc.sync.dma_start(out=wb_raw[:], in_=wb.rearrange("(p j) c -> p j c", j=PACK))
+            nc.sync.dma_start(out=page[t][:], in_=page_rows[:, t, :])
         wa_codes = keep.tile([P, 2 * N], U8, name="wa_codes", align_bytes=64)
         nc.sync.dma_start(out=wa_codes[:].bitcast(I32), in_=wa_words[0].bitcast(I32))
         for q in range(4):
@@ -111,8 +115,17 @@ def tile_list_recipe_taste_store_kernel(
             nc.sync.dma_start(out=appeal_cols[:], in_=appeal.rearrange("(b p) -> p b", p=P))
 
         picked_scales = place([P, S], U8, "picked_scales", 26)
-        with tc.psum_pool(name="first_banks", bufs=4) as first_banks:
-            sums = [[first_banks.tile([P, BANK], F32, name="sum") for h in range(HALVES)] for t in range(PACK)]
+        with tc.psum_pool(name="first_banks", bufs=4) as first_banks, tc.psum_pool(name="turn", bufs=1) as turn:
+            identity = keep.tile([P, P], F32, name="identity")
+            make_identity(nc, identity[:])
+            turned = turn.tile([P, BANK // P, P], F32, name="turned")
+            for k in range(BANK // P):
+                nc.tensor.transpose(turned[:, k, :], first_rows[:, k * P : (k + 1) * P], identity[:])
+            halves = [slice(h * BANK, (h + 1) * BANK) for h in range(HALVES)]
+            quarters = [slice(0, BANK // 2), slice(BANK // 2, BANK)]
+            sum_order = [(0, cols) for cols in quarters] + [(1, halves[0]), (0, halves[1]), (1, halves[1])]
+            sum_order = sum_order + [(t, cols) for t in range(2, PACK) for cols in halves]
+            sums = [first_banks.tile([P, BANK], F32, name="sum")[:, : cols.stop - cols.start] for t, cols in sum_order]
             grouped = [place([P, PACK * H], BF16, f"grouped{a}", kib) for a, kib in enumerate((0, 4, 20))]
             picked = [place([P, S], U32, f"picked{a}", kib) for a, kib in enumerate((76, 80, 21))]
 
@@ -129,12 +142,12 @@ def tile_list_recipe_taste_store_kernel(
                 nc.vector.quantize_mx(out=codes[:].bitcast(FP8X4), scales=plane[:], in_=grouped[a][:])
                 return codes, plane
 
-            def multiply(a, t, h):
+            def multiply(a, i):
+                t, cols = sum_order[i]
                 codes, plane = stationary[a]
                 rows = slice(t * P, (t + 1) * P)
-                cols = slice(h * BANK, (h + 1) * BANK)
                 nc.tensor.matmul_mx(
-                    out=sums[t][h][:],
+                    out=sums[i],
                     lhsT=codes[:, rows].bitcast(FP8X4),
                     lhsT_scale=plane[:, rows],
                     rhs=picked[a][:, cols].bitcast(FP8X4),
@@ -149,23 +162,29 @@ def tile_list_recipe_taste_store_kernel(
                 round_w1(a)
                 if a == 0:
                     stationary.append(quantize_w1(0, keep.tile([P, H], U32, name="w1_codes0", align_bytes=64)))
+            spread = place([P, BANK // P, 4, 32], F32, "spread", 48)
+            nc.scalar.copy(out=spread[:], in_=turned[:, :, 0:P:PACK].unsqueeze(2).to_broadcast([P, BANK // P, 4, 32]))
+            first_weights = turn.tile([P, BANK], F32, name="first_weights")
+            for k in range(BANK // P):
+                nc.tensor.transpose(
+                    first_weights[:, k * P : (k + 1) * P], spread[:, k].rearrange("p g q -> p (g q)"), identity[:]
+                )
             nc.vector.tensor_copy(out=picked_scales[:], in_=table_scales[:].indirect(picks[:]))
             round_w1(2)
             stationary.append(quantize_w1(1, place([P, H], U32, "held_codes", 64)))
             stationary.append(quantize_w1(2, keep.tile([P, H], U32, name="w1_codes2", align_bytes=64)))
-            early_sums = [(t, h) for t in range(PACK // 2) for h in range(HALVES)]
             for a in range(PASSES - 1):
-                for t, h in early_sums:
-                    multiply(a, t, h)
-            for h in range(HALVES):
-                cols = slice(h * BANK, (h + 1) * BANK)
+                for i in range(EARLY_SUMS):
+                    multiply(a, i)
+            for cols in quarters + halves[1:]:
                 nc.vector.tensor_copy(
                     out=picked[2][:, cols], in_=table[2][:].indirect(picks[:, cols.start // 16 : cols.stop // 16])
                 )
-            for t, h in early_sums:
-                multiply(PASSES - 1, t, h)
+            for i in range(EARLY_SUMS):
+                multiply(PASSES - 1, i)
 
-            woven = [place([P, PACK * BANK], BF16, f"woven{c}", kib) for c, kib in enumerate((74, 78, 82, 19))]
+            woven_all = place([P, PACK * T2], BF16, "woven", 70)
+            woven = [woven_all[:, c * PACK * BANK : (c + 1) * PACK * BANK] for c in range(CHUNKS)]
             out_rows = out_1.rearrange("(p t) c -> p t c", t=PACK)
             parts = []
             for c in range(CHUNKS):
@@ -173,9 +192,10 @@ def tile_list_recipe_taste_store_kernel(
                 parts = parts + [(c, lo, hi) for lo, hi in ((0, cut), (cut, BANK)) if hi > lo]
 
             def weave(t, c, lo, hi):
-                target = woven[c][:].rearrange("p (m t) -> p m t", t=PACK)[:, lo:hi]
-                source = page[t][:, c * BANK + lo : c * BANK + hi]
-                if c * BANK + lo >= VECTOR_COLS or t < PACK - 2:
+                cols = slice(c * BANK + lo, c * BANK + hi)
+                target = woven_all[:].rearrange("p (m t) -> p m t", t=PACK)[:, cols]
+                source = page[t][:, cols]
+                if cols.start >= VECTOR_COLS or t < PACK - 2:
                     nc.scalar.copy(out=target[:, :, t], in_=source)
                 elif t == PACK - 2:
                     nc.scalar.copy(out=target[:, :, t:], in_=source.unsqueeze(2).to_broadcast([P, hi - lo, 2]))
@@ -184,29 +204,48 @@ def tile_list_recipe_taste_store_kernel(
 
             factors = [keep.tile([P, S], F32, name=f"factor{t}") for t in range(PACK)]
             plain = [place([P, S], F32, f"plain{t}", 48 + 4 * t) for t in range(PACK)]
-            for t in range(PACK):
-                for h in range(HALVES):
-                    cols = slice(h * BANK, (h + 1) * BANK)
-                    if (t, h) not in early_sums:
-                        for a in range(PASSES):
-                            multiply(a, t, h)
-                    nc.scalar.activation(
-                        out=factors[t][:, cols], in_=sums[t][h][:], func=IDENTITY, bias=1.0, scale=curve_cols[:, t : t + 1]
-                    )
-                    if (t, h) != (0, 0):
-                        nc.scalar.copy(out=plain[t][:, cols], in_=sums[t][h][:])
+            for i, (t, cols) in enumerate(sum_order):
+                if i >= EARLY_SUMS:
+                    for a in range(PASSES):
+                        multiply(a, i)
+                nc.scalar.activation(
+                    out=factors[t][:, cols], in_=sums[i], func=IDENTITY, bias=1.0, scale=curve_cols[:, t : t + 1]
+                )
+                if i >= len(quarters):
+                    nc.scalar.copy(out=plain[t][:, cols], in_=sums[i])
 
             pieces = [(t, h * BANK, (h + 1) * BANK) for t in range(SPLIT_TILES) for h in range(HALVES)]
             pieces = pieces + [(t, 0, S) for t in range(SPLIT_TILES, PACK)]
-            values = [slots.tile([P, S], F32, name=f"value{t}", offset=4 * S * (PACK + 1 - t), align_bytes=64) for t in range(PACK)]
-            for i, (t, lo, hi) in enumerate(pieces):
-                state = slots.tile([P, hi - lo], F32, name=f"state{i}", offset=4 * S * (i == 0), align_bytes=64)
-                if i == 0:
-                    nc.vector.tensor_tensor(out=state[:], in0=sums[0][0][:], in1=factors[0][:, lo:hi], op=MULT)
-                    nc.vector.tensor_tensor(out=values[0][:, lo:hi], in0=state[:], in1=weights[0][:, lo:hi], op=MULT)
-                else:
-                    nc.gpsimd.tensor_tensor(out=state[:], in0=plain[t][:, lo:hi], in1=factors[t][:, lo:hi], op=MULT)
-                    nc.gpsimd.tensor_tensor(out=values[t][:, lo:hi], in0=state[:], in1=weights[t][:, lo:hi], op=MULT)
+            value_kib = (22, 20, 4, 18, 12, 8)
+            state_kib = (6, 4, 0, 0, 0, 0)
+            values = [
+                slots.tile([P, hi - lo], F32, name=f"value{i}", offset=value_kib[i] * KIB, align_bytes=64)
+                for i, (t, lo, hi) in enumerate(pieces)
+            ]
+            states = [
+                slots.tile([P, hi - lo], F32, name=f"state{i}", offset=state_kib[i] * KIB, align_bytes=64)
+                for i, (t, lo, hi) in enumerate(pieces)
+            ]
+
+            def curved(i):
+                t, lo, hi = pieces[i]
+                nc.gpsimd.tensor_tensor(out=states[i][:], in0=plain[t][:, lo:hi], in1=factors[t][:, lo:hi], op=MULT)
+
+            def weighted(i):
+                t, lo, hi = pieces[i]
+                nc.gpsimd.tensor_tensor(out=values[i][:], in0=states[i][:], in1=weights[t][:, lo:hi], op=MULT)
+
+            for k, part in enumerate(quarters):
+                nc.vector.tensor_tensor(out=states[0][:, part], in0=sums[k], in1=factors[0][:, part], op=MULT)
+            for part in quarters:
+                nc.vector.tensor_tensor(out=values[0][:, part], in0=first_weights[:, part], in1=states[0][:, part], op=MULT)
+            curved(2)
+            curved(1)
+            weighted(1)
+            weighted(2)
+            for i in range(3, len(pieces)):
+                curved(i)
+                weighted(i)
         psum = ctx.enter_context(tc.psum_pool(name="psum", bufs=8))
         wb_grouped = slots.tile([P, PACK * N], BF16, name="wb_grouped", offset=0, align_bytes=64)
         nc.gpsimd.tensor_scalar(
@@ -218,16 +257,15 @@ def tile_list_recipe_taste_store_kernel(
             op1=ADD,
         )
 
-        for t, lo, hi in pieces:
-            nc.vector.tensor_copy(out=page[t][:].indirect(places[:, lo // 16 : hi // 16]), in_=values[t][:, lo:hi])
+        for i, (t, lo, hi) in enumerate(pieces):
+            nc.vector.tensor_copy(out=page[t][:].indirect(places[:, lo // 16 : hi // 16]), in_=values[i][:])
             if hi == S:
                 nc.sync.dma_start(out=out_rows[:, t, :], in_=page[t][:])
                 if t < PACK - 2:
-                    for c in range(CHUNKS):
-                        weave(t, c, 0, BANK)
+                    weave(t, 0, 0, T2)
                 if t == PACK - 2:
-                    for part in parts:
-                        weave(t, *part)
+                    weave(t, 0, 0, VECTOR_COLS)
+                    weave(t, 0, VECTOR_COLS, T2)
 
         page_codes = keep.tile([P, T2], U32, name="page_codes", align_bytes=64)
         page_plane = keep.tile([P, T2], U8, name="page_plane", align_bytes=64)
@@ -236,7 +274,7 @@ def tile_list_recipe_taste_store_kernel(
 
         def quantize_page(c):
             cols = slice(c * BANK, (c + 1) * BANK)
-            nc.vector.quantize_mx(out=page_codes[:, cols].bitcast(FP8X4), scales=page_plane[:, cols], in_=woven[c][:])
+            nc.vector.quantize_mx(out=page_codes[:, cols].bitcast(FP8X4), scales=page_plane[:, cols], in_=woven[c])
             nc.sync.dma_start(out=words_out[:, cols], in_=page_codes[:, cols].bitcast(I32))
 
         def fit_slot(index):

@@ -30,10 +30,10 @@ UNITS = CHUNKS * BLOCKS
 KIB = 1024
 VECTOR_COLS = 1024
 W1_VECTOR = 84
-SCALAR_ADDS = (4, 9, 14)
-ADD_LAG = 2
+SCALAR_ADDS = (4, 9, 13, 14)
+FIT_LEAD = 3
 EARLY_SUMS = 4
-SPLIT_TILES = 2
+GAP_SUM = 4
 
 
 def tile_list_recipe_taste_store_kernel(
@@ -211,13 +211,12 @@ def tile_list_recipe_taste_store_kernel(
                 nc.scalar.activation(
                     out=factors[t][:, cols], in_=sums[i], func=IDENTITY, bias=1.0, scale=curve_cols[:, t : t + 1]
                 )
-                if i >= len(quarters):
+                if i >= len(quarters) and i != GAP_SUM:
                     nc.scalar.copy(out=plain[t][:, cols], in_=sums[i])
 
-            pieces = [(t, h * BANK, (h + 1) * BANK) for t in range(SPLIT_TILES) for h in range(HALVES)]
-            pieces = pieces + [(t, 0, S) for t in range(SPLIT_TILES, PACK)]
-            value_kib = (22, 20, 4, 18, 12, 8)
-            state_kib = (6, 4, 0, 0, 0, 0)
+            pieces = [(0, 0, BANK), (0, BANK, S)] + [(t, 0, S) for t in range(1, PACK)]
+            value_kib = (22, 20, 16, 12, 8)
+            state_kib = (6, 0, 4, 4, 4)
             values = [
                 slots.tile([P, hi - lo], F32, name=f"value{i}", offset=value_kib[i] * KIB, align_bytes=64)
                 for i, (t, lo, hi) in enumerate(pieces)
@@ -227,27 +226,34 @@ def tile_list_recipe_taste_store_kernel(
                 for i, (t, lo, hi) in enumerate(pieces)
             ]
 
-            def curved(i):
-                t, lo, hi = pieces[i]
-                nc.gpsimd.tensor_tensor(out=states[i][:], in0=plain[t][:, lo:hi], in1=factors[t][:, lo:hi], op=MULT)
+            def curved(i, lo, hi):
+                t, first = pieces[i][:2]
+                part = states[i][:, lo - first : hi - first]
+                nc.gpsimd.tensor_tensor(out=part, in0=plain[t][:, lo:hi], in1=factors[t][:, lo:hi], op=MULT)
 
             def weighted(i):
                 t, lo, hi = pieces[i]
                 nc.gpsimd.tensor_tensor(out=values[i][:], in0=states[i][:], in1=weights[t][:, lo:hi], op=MULT)
 
+            def scatter(i):
+                t, lo, hi = pieces[i]
+                nc.vector.tensor_copy(out=page[t][:].indirect(places[:, lo // 16 : hi // 16]), in_=values[i][:])
+
             for k, part in enumerate(quarters):
                 nc.vector.tensor_tensor(out=states[0][:, part], in0=sums[k], in1=factors[0][:, part], op=MULT)
             for part in quarters:
                 nc.vector.tensor_tensor(out=values[0][:, part], in0=first_weights[:, part], in1=states[0][:, part], op=MULT)
-            curved(2)
-            curved(1)
+            scatter(0)
+            curved(2, 0, BANK)
+            nc.vector.tensor_tensor(out=states[2][:, BANK:], in0=sums[GAP_SUM], in1=factors[1][:, BANK:], op=MULT)
+            curved(1, BANK, S)
             weighted(1)
             weighted(2)
             for i in range(3, len(pieces)):
-                curved(i)
+                curved(i, 0, S)
                 weighted(i)
         psum = ctx.enter_context(tc.psum_pool(name="psum", bufs=8))
-        wb_grouped = slots.tile([P, PACK * N], BF16, name="wb_grouped", offset=0, align_bytes=64)
+        wb_grouped = slots.tile([P, PACK * N], BF16, name="wb_grouped", offset=4 * KIB, align_bytes=64)
         nc.gpsimd.tensor_scalar(
             out=wb_grouped[:].rearrange("p (c i j) -> p c j i", i=PACK, j=PACK),
             in0=wb_raw[:].rearrange("p j (c i) -> p c j i", i=PACK),
@@ -258,7 +264,8 @@ def tile_list_recipe_taste_store_kernel(
         )
 
         for i, (t, lo, hi) in enumerate(pieces):
-            nc.vector.tensor_copy(out=page[t][:].indirect(places[:, lo // 16 : hi // 16]), in_=values[i][:])
+            if i >= 1:
+                scatter(i)
             if hi == S:
                 nc.sync.dma_start(out=out_rows[:, t, :], in_=page[t][:])
                 if t < PACK - 2:
@@ -280,10 +287,9 @@ def tile_list_recipe_taste_store_kernel(
         def fit_slot(index):
             return 86 + 2 * index
 
-        def products(index, c, b):
+        def fit_pass(index, c, b):
             cols = slice(c * BANK, (c + 1) * BANK)
             fit = psum.tile([P, BANK], F32, name="bank")
-            want = psum.tile([P, BANK], F32, name="bank")
             nc.tensor.matmul_mx(
                 out=fit[:],
                 lhsT=wa_codes[:, 2 * b * P : 2 * (b + 1) * P].bitcast(FP4X4),
@@ -293,6 +299,13 @@ def tile_list_recipe_taste_store_kernel(
                 start=True,
                 stop=True,
             )
+            fit_copy = place([P, BANK], F32, f"fit_copy{index}", fit_slot(index))
+            nc.scalar.copy(out=fit_copy[:], in_=fit[:])
+            return fit_copy
+
+        def product(index, c, b, fit_copy):
+            cols = slice(c * BANK, (c + 1) * BANK)
+            want = psum.tile([P, BANK], F32, name="bank")
             nc.tensor.matmul_mx(
                 out=want[:],
                 lhsT=wb_codes[:, b * P : (b + 1) * P].bitcast(FP8X4),
@@ -302,8 +315,6 @@ def tile_list_recipe_taste_store_kernel(
                 start=True,
                 stop=True,
             )
-            fit_copy = place([P, BANK], F32, f"fit_copy{index}", fit_slot(index))
-            nc.scalar.copy(out=fit_copy[:], in_=fit[:])
             score = place([P, BANK], F32, f"score{index}", 2 * index if index < 8 else 16 + 2 * index)
             nc.vector.tensor_tensor(out=score[:], in0=want[:], in1=fit_copy[:], op=MULT)
             return score
@@ -312,12 +323,8 @@ def tile_list_recipe_taste_store_kernel(
             bias = appeal_cols[:, b : b + 1]
             if index == UNITS - 1:
                 nc.vector.tensor_scalar(out=score[:], in0=score[:], scalar1=bias, scalar2=None, op0=ADD)
-            elif index == UNITS - 2:
-                nc.scalar.activation(out=score[:], in_=score[:], func=IDENTITY, bias=bias)
             elif index in SCALAR_ADDS:
-                biased = place([P, BANK], F32, f"biased{index}", fit_slot(index + ADD_LAG))
-                nc.scalar.activation(out=biased[:], in_=score[:], func=IDENTITY, bias=bias)
-                score = biased
+                nc.scalar.activation(out=score[:], in_=score[:], func=IDENTITY, bias=bias)
             else:
                 nc.gpsimd.tensor_scalar(out=score[:], in0=score[:], scalar1=1.0, scalar2=bias, op0=MULT, op1=ADD)
             nc.sync.dma_start(out=score_rows[:, b, c * BANK : (c + 1) * BANK], in_=score[:])
@@ -339,14 +346,12 @@ def tile_list_recipe_taste_store_kernel(
             quantize_page(c)
         score_units = [(c, b) for c in order for b in range(BLOCKS)]
         scores = []
+        fits = [fit_pass(index, *score_units[index]) for index in range(FIT_LEAD)]
         for index, (c, b) in enumerate(score_units):
-            scores.append(products(index, c, b))
-            if index >= 1 and index - 1 not in SCALAR_ADDS:
-                finish(index - 1, *score_units[index - 1], scores[index - 1])
-            if index - ADD_LAG in SCALAR_ADDS:
-                finish(index - ADD_LAG, *score_units[index - ADD_LAG], scores[index - ADD_LAG])
-        for index in (UNITS - 2, UNITS - 1):
-            finish(index, *score_units[index], scores[index])
+            if index + FIT_LEAD < UNITS:
+                fits.append(fit_pass(index + FIT_LEAD, *score_units[index + FIT_LEAD]))
+            scores.append(product(index, c, b, fits[index]))
+            finish(index, c, b, scores[index])
         for q in range(4):
             nc.sync.dma_start(
                 out=out_3[0, 4 * q : 4 * q + 4, :].bitcast(I32), in_=page_plane[32 * q : 32 * q + 4, :].bitcast(I32)

@@ -33,7 +33,9 @@ W1_VECTOR = 84
 SCALAR_ADDS = (4, 9, 13, 14)
 FIT_LEAD = 3
 EARLY_SUMS = 4
-GAP_SUM = 4
+FILL = 256
+DIRECT = 1024
+FILL_SUM = 2
 
 
 def tile_list_recipe_taste_store_kernel(
@@ -96,8 +98,11 @@ def tile_list_recipe_taste_store_kernel(
         nc.vector.memset(wa_plane[:].bitcast(I32), 0)
         nc.sync.dma_start(out=page[0][:], in_=page_rows[:, 0, :])
         nc.sync.dma_start(places[:], offs2)
+        load_weights(1, slice(0, FILL))
+        nc.sync.dma_start(out=page[1][:], in_=page_rows[:, 1, :])
         load_weights(0, slice(BANK, S))
-        for t in range(1, PACK):
+        load_weights(1, slice(FILL, S))
+        for t in range(2, PACK):
             load_weights(t, slice(0, S))
             if t == PACK - 1:
                 wb_raw = keep.tile([P, PACK, N], F32, name="wb_raw")
@@ -211,12 +216,14 @@ def tile_list_recipe_taste_store_kernel(
                 nc.scalar.activation(
                     out=factors[t][:, cols], in_=sums[i], func=IDENTITY, bias=1.0, scale=curve_cols[:, t : t + 1]
                 )
-                if i >= len(quarters) and i != GAP_SUM:
+                if i == FILL_SUM:
+                    nc.scalar.copy(out=plain[t][:, FILL:BANK], in_=sums[i][:, FILL:])
+                if i > FILL_SUM:
                     nc.scalar.copy(out=plain[t][:, cols], in_=sums[i])
 
-            pieces = [(0, 0, BANK), (0, BANK, S)] + [(t, 0, S) for t in range(1, PACK)]
-            value_kib = (22, 20, 16, 12, 8)
-            state_kib = (6, 0, 4, 4, 4)
+            pieces = [(0, 0, BANK), (1, 0, FILL), (0, BANK, S), (1, FILL, S)] + [(t, 0, S) for t in range(2, PACK)]
+            value_kib = (22, 21, 19, 16, 12, 8)
+            state_kib = (0, 4, 4, 4, 4, 4)
             values = [
                 slots.tile([P, hi - lo], F32, name=f"value{i}", offset=value_kib[i] * KIB, align_bytes=64)
                 for i, (t, lo, hi) in enumerate(pieces)
@@ -243,14 +250,11 @@ def tile_list_recipe_taste_store_kernel(
                 nc.vector.tensor_tensor(out=states[0][:, part], in0=sums[k], in1=factors[0][:, part], op=MULT)
             for part in quarters:
                 nc.vector.tensor_tensor(out=values[0][:, part], in0=first_weights[:, part], in1=states[0][:, part], op=MULT)
+            nc.vector.tensor_tensor(out=states[1][:], in0=sums[FILL_SUM][:, :FILL], in1=factors[1][:, :FILL], op=MULT)
             scatter(0)
-            curved(2, 0, BANK)
-            nc.vector.tensor_tensor(out=states[2][:, BANK:], in0=sums[GAP_SUM], in1=factors[1][:, BANK:], op=MULT)
-            curved(1, BANK, S)
             weighted(1)
-            weighted(2)
-            for i in range(3, len(pieces)):
-                curved(i, 0, S)
+            for i in range(2, len(pieces)):
+                curved(i, *pieces[i][1:])
                 weighted(i)
         psum = ctx.enter_context(tc.psum_pool(name="psum", bufs=8))
         wb_grouped = slots.tile([P, PACK * N], BF16, name="wb_grouped", offset=4 * KIB, align_bytes=64)
@@ -263,13 +267,20 @@ def tile_list_recipe_taste_store_kernel(
             op1=ADD,
         )
 
+        pairs = place([P, 2 * (T2 - DIRECT)], BF16, "pairs", 21)
         for i, (t, lo, hi) in enumerate(pieces):
             if i >= 1:
                 scatter(i)
             if hi == S:
                 nc.sync.dma_start(out=out_rows[:, t, :], in_=page[t][:])
                 if t < PACK - 2:
-                    weave(t, 0, 0, T2)
+                    nc.scalar.copy(out=pairs[:].rearrange("p (m e) -> p m e", e=2)[:, :, t], in_=page[t][:, DIRECT:])
+                    weave(t, 0, 0, DIRECT)
+                if t == 1:
+                    nc.scalar.copy(
+                        out=woven_all[:].bitcast(F32).rearrange("p (m u) -> p m u", u=2)[:, DIRECT:],
+                        in_=pairs[:].bitcast(F32).unsqueeze(2).to_broadcast([P, T2 - DIRECT, 2]),
+                    )
                 if t == PACK - 2:
                     weave(t, 0, 0, VECTOR_COLS)
                     weave(t, 0, VECTOR_COLS, T2)

@@ -78,7 +78,7 @@ def tile_list_recipe_taste_store_kernel(
         wgs_rows = wgs.rearrange("(q t) j -> q t j", t=PACK)
         first_rows = keep.tile([P, BANK], F32, name="first_rows")
         nc.vector.memset(first_rows[:], 0.0)
-        nc.sync.dma_start(out=first_rows[0:P:PACK, :], in_=wgs_rows[:, 0, 0:BANK])
+        nc.sync.dma_start(out=first_rows[0:P:2, :], in_=wgs_rows[:, 0:2, 0:BANK])
         load_table(1)
         load_w1(1)
         load_w1(2)
@@ -98,10 +98,9 @@ def tile_list_recipe_taste_store_kernel(
         nc.vector.memset(wa_plane[:].bitcast(I32), 0)
         nc.sync.dma_start(out=page[0][:], in_=page_rows[:, 0, :])
         nc.sync.dma_start(places[:], offs2)
-        load_weights(1, slice(0, FILL))
         nc.sync.dma_start(out=page[1][:], in_=page_rows[:, 1, :])
         load_weights(0, slice(BANK, S))
-        load_weights(1, slice(FILL, S))
+        load_weights(1, slice(BANK, S))
         for t in range(2, PACK):
             load_weights(t, slice(0, S))
             if t == PACK - 1:
@@ -167,13 +166,18 @@ def tile_list_recipe_taste_store_kernel(
                 round_w1(a)
                 if a == 0:
                     stationary.append(quantize_w1(0, keep.tile([P, H], U32, name="w1_codes0", align_bytes=64)))
-            spread = place([P, BANK // P, 4, 32], F32, "spread", 48)
-            nc.scalar.copy(out=spread[:], in_=turned[:, :, 0:P:PACK].unsqueeze(2).to_broadcast([P, BANK // P, 4, 32]))
-            first_weights = turn.tile([P, BANK], F32, name="first_weights")
-            for k in range(BANK // P):
-                nc.tensor.transpose(
-                    first_weights[:, k * P : (k + 1) * P], spread[:, k].rearrange("p g q -> p (g q)"), identity[:]
-                )
+            dealt = []
+            for t in range(2):
+                spread = place([P, BANK // P, 4, 32], F32, f"spread{t}", 48 + 2 * t)
+                rows = turned[:, :, 2 * t : P : PACK]
+                nc.scalar.copy(out=spread[:], in_=rows.unsqueeze(2).to_broadcast([P, BANK // P, 4, 32]))
+                dealt.append(turn.tile([P, BANK], F32, name=f"dealt{t}"))
+                for k in range(BANK // P):
+                    nc.tensor.transpose(
+                        dealt[t][:, k * P : (k + 1) * P], spread[:, k].rearrange("p g q -> p (g q)"), identity[:]
+                    )
+            first_weights = dealt[0]
+            nc.scalar.copy(out=weights[1][:, halves[0]], in_=dealt[1][:])
             nc.vector.tensor_copy(out=picked_scales[:], in_=table_scales[:].indirect(picks[:]))
             round_w1(2)
             stationary.append(quantize_w1(1, place([P, H], U32, "held_codes", 64)))
@@ -213,9 +217,15 @@ def tile_list_recipe_taste_store_kernel(
                 if i >= EARLY_SUMS:
                     for a in range(PASSES):
                         multiply(a, i)
-                nc.scalar.activation(
-                    out=factors[t][:, cols], in_=sums[i], func=IDENTITY, bias=1.0, scale=curve_cols[:, t : t + 1]
-                )
+                width = cols.stop - cols.start
+                for lo, hi in ((0, FILL), (FILL, width)) if i == FILL_SUM else ((0, width),):
+                    nc.scalar.activation(
+                        out=factors[t][:, cols.start + lo : cols.start + hi],
+                        in_=sums[i][:, lo:hi],
+                        func=IDENTITY,
+                        bias=1.0,
+                        scale=curve_cols[:, t : t + 1],
+                    )
                 if i == FILL_SUM:
                     nc.scalar.copy(out=plain[t][:, FILL:BANK], in_=sums[i][:, FILL:])
                 if i > FILL_SUM:

from contextlib import ExitStack

import concourse.mybir as mybir
from concourse.masks import make_identity

K, T, S, H, T2, N = 1536, 4096, 1024, 512, 2048, 512
FLOPS = 2 * K * H * S + 2 * 2 * H * N * T2

F32 = mybir.dt.float32
BF16 = mybir.dt.bfloat16
I32 = mybir.dt.int32
U32 = mybir.dt.uint32
U16 = mybir.dt.uint16
U8 = mybir.dt.uint8
FP8X4 = mybir.dt.float8_e4m3fn_x4
FP4X4 = mybir.dt.float4_e2m1fn_x4
MULT = mybir.AluOpType.mult
ADD = mybir.AluOpType.add
IDENTITY = mybir.ActivationFunctionType.Identity

P = 128
PACK = 4
K_PASS = P * PACK
PASSES = K // K_PASS
BANK = 512
HALVES = S // BANK
CHUNKS = T2 // BANK
BLOCKS = N // P
UNITS = CHUNKS * BLOCKS
KIB = 1024
VECTOR_COLS = 1024
W1_VECTOR = 84
SCALAR_ADDS = (4, 9, 13, 14)
FIT_LEAD = 3
EARLY_SUMS = 4
FILL = 256
DIRECT = 1024
FILL_SUM = 2


def tile_list_recipe_taste_store_kernel(
    tc, tab_words, tab_scales, offs, offs2, w1, curve, wgs, page0, wa_words, wa_scales, wb, appeal,
    out_0, out_1, out_2, out_3,
):
    nc = tc.nc
    with ExitStack() as ctx:
        keep = ctx.enter_context(tc.tile_pool(name="keep", bufs=1))
        arena = ctx.enter_context(tc.tile_pool(name="arena", bufs=1))
        slots = ctx.enter_context(tc.tile_pool(name="slots", bufs=1))

        def place(shape, dtype, name, kib):
            return arena.tile(shape, dtype, name=name, offset=kib * KIB, align_bytes=64)

        picks = keep.tile([P, S // 16], U16, name="picks")
        places = keep.tile([P, S // 16], U16, name="places")

        table_scales = place([P, T], U8, "table_scales", 72)
        nc.vector.memset(table_scales[:].bitcast(I32), 0)
        table = [place([P, T], U32, f"table{a}", 16 * a) for a in range(PASSES)]
        w1_raw = [place([P, PACK, H], F32, f"w1_raw{a}", 48 + 8 * a) for a in range(PASSES)]

        def load_table(a):
            words = tab_words[a].rearrange("p n t -> p (n t)").bitcast(I32)
            nc.sync.dma_start(out=table[a][:].bitcast(I32), in_=words)

        def load_w1(a):
            rows = w1[a * K_PASS : (a + 1) * K_PASS, :].rearrange("(p j) c -> p j c", j=PACK)
            nc.sync.dma_start(out=w1_raw[a][:], in_=rows)

        load_table(0)
        nc.sync.dma_start(picks[:], offs)
        for q in range(4):
            nc.gpsimd.dma_start(
                out=table_scales[32 * q : 32 * q + 4 * PASSES, :].bitcast(I32),
                in_=tab_scales[:, 4 * q : 4 * q + 4, :].bitcast(I32),
            )
        load_w1(0)
        wgs_rows = wgs.rearrange("(q t) j -> q t j", t=PACK)
        first_rows = keep.tile([P, BANK], F32, name="first_rows")
        nc.vector.memset(first_rows[:], 0.0)
        nc.sync.dma_start(out=first_rows[0:P:2, :], in_=wgs_rows[:, 0:2, 0:BANK])
        load_table(1)
        load_w1(1)
        load_w1(2)
        load_table(2)
        curve_cols = keep.tile([P, PACK], F32, name="curve_cols")
        nc.sync.dma_start(out=curve_cols[:], in_=curve.rearrange("(p t) -> p t", t=PACK))

        page_rows = page0.rearrange("(p t) c -> p t c", t=PACK)
        page = [keep.tile([P, T2], F32, name=f"page{t}") for t in range(PACK)]
        weights = [keep.tile([P, S], F32, name=f"weights{t}") for t in range(PACK)]

        def load_weights(t, cols):
            for q in (0, 2, 1, 3):
                nc.sync.dma_start(out=weights[t][32 * q : 32 * q + 32, cols], in_=wgs_rows[:, t, cols])

        wa_plane = keep.tile([P, N], U8, name="wa_plane", align_bytes=64)
        nc.vector.memset(wa_plane[:].bitcast(I32), 0)
        nc.sync.dma_start(out=page[0][:], in_=page_rows[:, 0, :])
        nc.sync.dma_start(places[:], offs2)
        nc.sync.dma_start(out=page[1][:], in_=page_rows[:, 1, :])
        load_weights(0, slice(BANK, S))
        load_weights(1, slice(BANK, S))
        for t in range(2, PACK):
            load_weights(t, slice(0, S))
            if t == PACK - 1:
                wb_raw = keep.tile([P, PACK, N], F32, name="wb_raw")
                nc.sync.dma_start(out=wb_raw[:], in_=wb.rearrange("(p j) c -> p j c", j=PACK))
            nc.sync.dma_start(out=page[t][:], in_=page_rows[:, t, :])
        wa_codes = keep.tile([P, 2 * N], U8, name="wa_codes", align_bytes=64)
        nc.sync.dma_start(out=wa_codes[:].bitcast(I32), in_=wa_words[0].bitcast(I32))
        for q in range(4):
            nc.sync.dma_start(
                out=wa_plane[32 * q : 32 * q + 4, :].bitcast(I32),
                in_=wa_scales[0, 4 * q : 4 * q + 4, :].bitcast(I32),
            )
        appeal_cols = keep.tile([P, BLOCKS], F32, name="appeal_cols")
        with nc.allow_non_contiguous_dma(reason="one bias value for each partition"):
            nc.sync.dma_start(out=appeal_cols[:], in_=appeal.rearrange("(b p) -> p b", p=P))

        picked_scales = place([P, S], U8, "picked_scales", 26)
        with tc.psum_pool(name="first_banks", bufs=4) as first_banks, tc.psum_pool(name="turn", bufs=1) as turn:
            identity = keep.tile([P, P], F32, name="identity")
            make_identity(nc, identity[:])
            turned = turn.tile([P, BANK // P, P], F32, name="turned")
            for k in range(BANK // P):
                nc.tensor.transpose(turned[:, k, :], first_rows[:, k * P : (k + 1) * P], identity[:])
            halves = [slice(h * BANK, (h + 1) * BANK) for h in range(HALVES)]
            quarters = [slice(0, BANK // 2), slice(BANK // 2, BANK)]
            sum_order = [(0, cols) for cols in quarters] + [(1, halves[0]), (0, halves[1]), (1, halves[1])]
            sum_order = sum_order + [(t, cols) for t in range(2, PACK) for cols in halves]
            sums = [first_banks.tile([P, BANK], F32, name="sum")[:, : cols.stop - cols.start] for t, cols in sum_order]
            grouped = [place([P, PACK * H], BF16, f"grouped{a}", kib) for a, kib in enumerate((0, 4, 20))]
            picked = [place([P, S], U32, f"picked{a}", kib) for a, kib in enumerate((76, 80, 21))]

            def round_w1(a):
                dealt = grouped[a][:].rearrange("p (t m j) -> p m j t", t=PACK, j=PACK)
                loaded = w1_raw[a][:].rearrange("p j (m t) -> p m j t", t=PACK)
                share = W1_VECTOR if a == PASSES - 1 else 0
                nc.scalar.copy(out=dealt[:, share:], in_=loaded[:, share:])
                if share:
                    nc.vector.tensor_copy(out=dealt[:, :share], in_=loaded[:, :share])

            def quantize_w1(a, codes):
                plane = keep.tile([P, H], U8, name=f"w1_plane{a}", align_bytes=64)
                nc.vector.quantize_mx(out=codes[:].bitcast(FP8X4), scales=plane[:], in_=grouped[a][:])
                return codes, plane

            def multiply(a, i):
                t, cols = sum_order[i]
                codes, plane = stationary[a]
                rows = slice(t * P, (t + 1) * P)
                nc.tensor.matmul_mx(
                    out=sums[i],
                    lhsT=codes[:, rows].bitcast(FP8X4),
                    lhsT_scale=plane[:, rows],
                    rhs=picked[a][:, cols].bitcast(FP8X4),
                    rhs_scale=picked_scales[4 * a : P, cols],
                    start=(a == 0),
                    stop=(a == PASSES - 1),
                )

            stationary = []
            for a in range(PASSES - 1):
                nc.vector.tensor_copy(out=picked[a][:], in_=table[a][:].indirect(picks[:]))
                round_w1(a)
                if a == 0:
                    stationary.append(quantize_w1(0, keep.tile([P, H], U32, name="w1_codes0", align_bytes=64)))
            dealt = []
            for t in range(2):
                spread = place([P, BANK // P, 4, 32], F32, f"spread{t}", 48 + 2 * t)
                rows = turned[:, :, 2 * t : P : PACK]
                nc.scalar.copy(out=spread[:], in_=rows.unsqueeze(2).to_broadcast([P, BANK // P, 4, 32]))
                dealt.append(turn.tile([P, BANK], F32, name=f"dealt{t}"))
                for k in range(BANK // P):
                    nc.tensor.transpose(
                        dealt[t][:, k * P : (k + 1) * P], spread[:, k].rearrange("p g q -> p (g q)"), identity[:]
                    )
            first_weights = dealt[0]
            nc.scalar.copy(out=weights[1][:, halves[0]], in_=dealt[1][:])
            nc.vector.tensor_copy(out=picked_scales[:], in_=table_scales[:].indirect(picks[:]))
            round_w1(2)
            stationary.append(quantize_w1(1, place([P, H], U32, "held_codes", 64)))
            stationary.append(quantize_w1(2, keep.tile([P, H], U32, name="w1_codes2", align_bytes=64)))
            for a in range(PASSES - 1):
                for i in range(EARLY_SUMS):
                    multiply(a, i)
            for cols in quarters + halves[1:]:
                nc.vector.tensor_copy(
                    out=picked[2][:, cols], in_=table[2][:].indirect(picks[:, cols.start // 16 : cols.stop // 16])
                )
            for i in range(EARLY_SUMS):
                multiply(PASSES - 1, i)

            woven_all = place([P, PACK * T2], BF16, "woven", 70)
            woven = [woven_all[:, c * PACK * BANK : (c + 1) * PACK * BANK] for c in range(CHUNKS)]
            out_rows = out_1.rearrange("(p t) c -> p t c", t=PACK)
            parts = []
            for c in range(CHUNKS):
                cut = min(max(VECTOR_COLS - c * BANK, 0), BANK)
                parts = parts + [(c, lo, hi) for lo, hi in ((0, cut), (cut, BANK)) if hi > lo]

            def weave(t, c, lo, hi):
                cols = slice(c * BANK + lo, c * BANK + hi)
                target = woven_all[:].rearrange("p (m t) -> p m t", t=PACK)[:, cols]
                source = page[t][:, cols]
                if cols.start >= VECTOR_COLS or t < PACK - 2:
                    nc.scalar.copy(out=target[:, :, t], in_=source)
                elif t == PACK - 2:
                    nc.scalar.copy(out=target[:, :, t:], in_=source.unsqueeze(2).to_broadcast([P, hi - lo, 2]))
                else:
                    nc.vector.tensor_copy(out=target[:, :, t], in_=source)

            factors = [keep.tile([P, S], F32, name=f"factor{t}") for t in range(PACK)]
            plain = [place([P, S], F32, f"plain{t}", 48 + 4 * t) for t in range(PACK)]
            for i, (t, cols) in enumerate(sum_order):
                if i >= EARLY_SUMS:
                    for a in range(PASSES):
                        multiply(a, i)
                width = cols.stop - cols.start
                for lo, hi in ((0, FILL), (FILL, width)) if i == FILL_SUM else ((0, width),):
                    nc.scalar.activation(
                        out=factors[t][:, cols.start + lo : cols.start + hi],
                        in_=sums[i][:, lo:hi],
                        func=IDENTITY,
                        bias=1.0,
                        scale=curve_cols[:, t : t + 1],
                    )
                if i == FILL_SUM:
                    nc.scalar.copy(out=plain[t][:, FILL:BANK], in_=sums[i][:, FILL:])
                if i > FILL_SUM:
                    nc.scalar.copy(out=plain[t][:, cols], in_=sums[i])

            pieces = [(0, 0, BANK), (1, 0, FILL), (0, BANK, S), (1, FILL, S)] + [(t, 0, S) for t in range(2, PACK)]
            value_kib = (22, 21, 19, 16, 12, 8)
            state_kib = (0, 4, 4, 4, 4, 4)
            values = [
                slots.tile([P, hi - lo], F32, name=f"value{i}", offset=value_kib[i] * KIB, align_bytes=64)
                for i, (t, lo, hi) in enumerate(pieces)
            ]
            states = [
                slots.tile([P, hi - lo], F32, name=f"state{i}", offset=state_kib[i] * KIB, align_bytes=64)
                for i, (t, lo, hi) in enumerate(pieces)
            ]

            def curved(i, lo, hi):
                t, first = pieces[i][:2]
                part = states[i][:, lo - first : hi - first]
                nc.gpsimd.tensor_tensor(out=part, in0=plain[t][:, lo:hi], in1=factors[t][:, lo:hi], op=MULT)

            def weighted(i):
                t, lo, hi = pieces[i]
                nc.gpsimd.tensor_tensor(out=values[i][:], in0=states[i][:], in1=weights[t][:, lo:hi], op=MULT)

            def scatter(i):
                t, lo, hi = pieces[i]
                nc.vector.tensor_copy(out=page[t][:].indirect(places[:, lo // 16 : hi // 16]), in_=values[i][:])

            for k, part in enumerate(quarters):
                nc.vector.tensor_tensor(out=states[0][:, part], in0=sums[k], in1=factors[0][:, part], op=MULT)
            for part in quarters:
                nc.vector.tensor_tensor(out=values[0][:, part], in0=first_weights[:, part], in1=states[0][:, part], op=MULT)
            nc.vector.tensor_tensor(out=states[1][:], in0=sums[FILL_SUM][:, :FILL], in1=factors[1][:, :FILL], op=MULT)
            scatter(0)
            weighted(1)
            for i in range(2, len(pieces)):
                curved(i, *pieces[i][1:])
                weighted(i)
        psum = ctx.enter_context(tc.psum_pool(name="psum", bufs=8))
        wb_grouped = slots.tile([P, PACK * N], BF16, name="wb_grouped", offset=4 * KIB, align_bytes=64)
        nc.gpsimd.tensor_scalar(
            out=wb_grouped[:].rearrange("p (c i j) -> p c j i", i=PACK, j=PACK),
            in0=wb_raw[:].rearrange("p j (c i) -> p c j i", i=PACK),
            scalar1=1.0,
            scalar2=0.0,
            op0=MULT,
            op1=ADD,
        )

        pairs = place([P, 2 * (T2 - DIRECT)], BF16, "pairs", 21)
        for i, (t, lo, hi) in enumerate(pieces):
            if i >= 1:
                scatter(i)
            if hi == S:
                nc.sync.dma_start(out=out_rows[:, t, :], in_=page[t][:])
                if t < PACK - 2:
                    nc.scalar.copy(out=pairs[:].rearrange("p (m e) -> p m e", e=2)[:, :, t], in_=page[t][:, DIRECT:])
                    weave(t, 0, 0, DIRECT)
                if t == 1:
                    nc.scalar.copy(
                        out=woven_all[:].bitcast(F32).rearrange("p (m u) -> p m u", u=2)[:, DIRECT:],
                        in_=pairs[:].bitcast(F32).unsqueeze(2).to_broadcast([P, T2 - DIRECT, 2]),
                    )
                if t == PACK - 2:
                    weave(t, 0, 0, VECTOR_COLS)
                    weave(t, 0, VECTOR_COLS, T2)

        page_codes = keep.tile([P, T2], U32, name="page_codes", align_bytes=64)
        page_plane = keep.tile([P, T2], U8, name="page_plane", align_bytes=64)
        words_out = out_2[0].rearrange("p m t -> p (m t)").bitcast(I32)
        score_rows = out_0.rearrange("(b p) c -> p b c", p=P)

        def quantize_page(c):
            cols = slice(c * BANK, (c + 1) * BANK)
            nc.vector.quantize_mx(out=page_codes[:, cols].bitcast(FP8X4), scales=page_plane[:, cols], in_=woven[c])
            nc.sync.dma_start(out=words_out[:, cols], in_=page_codes[:, cols].bitcast(I32))

        def fit_slot(index):
            return 86 + 2 * index

        def fit_pass(index, c, b):
            cols = slice(c * BANK, (c + 1) * BANK)
            fit = psum.tile([P, BANK], F32, name="bank")
            nc.tensor.matmul_mx(
                out=fit[:],
                lhsT=wa_codes[:, 2 * b * P : 2 * (b + 1) * P].bitcast(FP4X4),
                lhsT_scale=wa_plane[:, b * P : (b + 1) * P],
                rhs=page_codes[:, cols].bitcast(FP8X4),
                rhs_scale=page_plane[:, cols],
                start=True,
                stop=True,
            )
            fit_copy = place([P, BANK], F32, f"fit_copy{index}", fit_slot(index))
            nc.scalar.copy(out=fit_copy[:], in_=fit[:])
            return fit_copy

        def product(index, c, b, fit_copy):
            cols = slice(c * BANK, (c + 1) * BANK)
            want = psum.tile([P, BANK], F32, name="bank")
            nc.tensor.matmul_mx(
                out=want[:],
                lhsT=wb_codes[:, b * P : (b + 1) * P].bitcast(FP8X4),
                lhsT_scale=wb_plane[:, b * P : (b + 1) * P],
                rhs=page_codes[:, cols].bitcast(FP8X4),
                rhs_scale=page_plane[:, cols],
                start=True,
                stop=True,
            )
            score = place([P, BANK], F32, f"score{index}", 2 * index if index < 8 else 16 + 2 * index)
            nc.vector.tensor_tensor(out=score[:], in0=want[:], in1=fit_copy[:], op=MULT)
            return score

        def finish(index, c, b, score):
            bias = appeal_cols[:, b : b + 1]
            if index == UNITS - 1:
                nc.vector.tensor_scalar(out=score[:], in0=score[:], scalar1=bias, scalar2=None, op0=ADD)
            elif index in SCALAR_ADDS:
                nc.scalar.activation(out=score[:], in_=score[:], func=IDENTITY, bias=bias)
            else:
                nc.gpsimd.tensor_scalar(out=score[:], in0=score[:], scalar1=1.0, scalar2=bias, op0=MULT, op1=ADD)
            nc.sync.dma_start(out=score_rows[:, b, c * BANK : (c + 1) * BANK], in_=score[:])

        last = PACK - 1
        for c, lo, hi in parts:
            if c * BANK + lo >= VECTOR_COLS:
                weave(last, c, lo, hi)
        weave(last, *parts[0])
        wb_plane = keep.tile([P, N], U8, name="wb_plane", align_bytes=64)
        wb_codes = slots.tile([P, N], U32, name="wb_codes", offset=8 * S, align_bytes=64)
        nc.vector.quantize_mx(out=wb_codes[:].bitcast(FP8X4), scales=wb_plane[:], in_=wb_grouped[:])
        quantize_page(0)
        for c, lo, hi in parts[1:]:
            if c * BANK + lo < VECTOR_COLS:
                weave(last, c, lo, hi)
        order = (0, 2, 1, 3)
        for c in order[1:]:
            quantize_page(c)
        score_units = [(c, b) for c in order for b in range(BLOCKS)]
        scores = []
        fits = [fit_pass(index, *score_units[index]) for index in range(FIT_LEAD)]
        for index, (c, b) in enumerate(score_units):
            if index + FIT_LEAD < UNITS:
                fits.append(fit_pass(index + FIT_LEAD, *score_units[index + FIT_LEAD]))
            scores.append(product(index, c, b, fits[index]))
            finish(index, c, b, scores[index])
        for q in range(4):
            nc.sync.dma_start(
                out=out_3[0, 4 * q : 4 * q + 4, :].bitcast(I32), in_=page_plane[32 * q : 32 * q + 4, :].bitcast(I32)
            )
